import numpy as np
import ml_dtypes


def mxq(x, axis, fmt="e4m3"):
    dtype, down = {"e4m3": (ml_dtypes.float8_e4m3fn, 7), "e5m2": (ml_dtypes.float8_e5m2, 14)}[fmt]
    v = np.moveaxis(np.asarray(x, np.float32).astype(ml_dtypes.bfloat16).astype(np.float64), axis, -1)
    blocks = v.reshape(v.shape[:-1] + (-1, 32))
    amax = np.abs(blocks).max(-1, keepdims=True)
    byte = np.maximum(np.where(amax > 0, np.frexp(amax)[1] - 1 + 127, 0) - down, 1)
    scale = np.exp2(byte - 127.0)
    codes = (blocks / scale).astype(np.float32).astype(dtype).astype(np.float64)
    return np.moveaxis((codes * scale).reshape(v.shape), -1, axis)


WIDE = False


def mx_kscale(k):
    if not WIDE:
        return np.ones(k)
    levels = np.array([10, -10, 5, -5, 0])
    if k % 512:
        return np.exp2(np.random.permutation(np.resize(levels, k // 32))).repeat(32)
    a = np.empty((k // 512, 16))
    for p in range(k // 512):
        a[p, :8] = np.random.permutation(np.resize(levels, 8))
        for g in range(8):
            far = levels[np.abs(levels - a[p, g]) >= 10]
            a[p, g + 8] = far[np.random.randint(len(far))]
    return np.exp2(a.ravel()).repeat(32)


def f64(x):
    return np.asarray(x).astype(np.float64)


def striped(idx):
    return np.tile(idx.reshape(-1, 16).T, (8, 1)).astype(np.uint16)


def unstriped(offs):
    return offs[:16].T.reshape(-1).astype(np.int64)


E2M1 = np.array([0.0, 0.5, 1.0, 1.5, 2.0, 3.0, 4.0, 6.0, -0.0, -0.5, -1.0, -1.5, -2.0, -3.0, -4.0, -6.0])


def pack_weight(w, fmt):
    k, n = w.shape
    w = f64(np.asarray(w, np.float32).astype(ml_dtypes.bfloat16)).reshape(k // 32, 32, n)
    amax = np.abs(w).max(1)
    if fmt == "e4m3":
        byte = np.frexp(amax)[1] - 1 + 127 - 7
    else:
        mant, ex = np.frexp(amax / 6.0)
        byte = np.where(mant > 0.5, ex, ex - 1) + 127
    byte = np.clip(np.where(amax > 0, byte, 1), 1, 254)
    scaled = (w * np.exp2(127.0 - byte)[:, None, :]).reshape(k, n).astype(np.float32)
    by_word = np.ascontiguousarray(scaled.reshape(k // 512, 128, 4, n).transpose(0, 1, 3, 2))
    if fmt == "e4m3":
        words = by_word.astype(ml_dtypes.float8_e4m3fn).view(np.uint8)
    else:
        c = by_word.astype(ml_dtypes.float4_e2m1fn).view(np.uint8) & 0xF
        words = (c[..., 0::2] | (c[..., 1::2] << 4)).reshape(k // 512, 128, 2 * n)
    return np.ascontiguousarray(words), np.ascontiguousarray(byte.astype(np.uint8).reshape(k // 512, 16, n))


def unpack_weight(words, scales, fmt):
    g, _, n = scales.shape
    words = np.ascontiguousarray(words).reshape(g, 128, n, -1)
    if fmt == "e4m3":
        vals = words.view(ml_dtypes.float8_e4m3fn).astype(np.float64)
    else:
        nib = np.empty((g, 128, n, 4), np.uint8)
        nib[..., 0::2] = words & 0xF
        nib[..., 1::2] = words >> 4
        vals = E2M1[nib]
    vals = vals * np.repeat(np.exp2(scales.astype(np.float64) - 127.0), 8, axis=1)[..., None]
    return vals.transpose(0, 1, 3, 2).reshape(g * 512, n)


def gelu(v):
    return 0.5 * v * (1.0 + np.tanh(np.sqrt(2.0 / np.pi) * (v + 0.044715 * v**3)))


K, T, S, H, T2, N, P = 1536, 2048, 512, 1024, 1024, 768, 512

def setup_inputs():
    n = np.random.standard_normal
    s = mx_kscale(K)[:, None]
    u = mx_kscale(H)[:, None]
    d = {}
    d["tab_words"], d["tab_scales"] = pack_weight(n((K, T)) * s, "e4m3")
    d["wa"] = (n((K, H)) * 1.7 / K ** 0.5 / s).astype(np.float32)
    d["wd_words"], d["wd_scales"] = pack_weight(n((K, H)) * 1.2 / K ** 0.5 / s, "e2m1")
    d["gain"] = (3.0 * np.exp(0.2 * n(H)) * u[:, 0]).astype(np.float32)
    d["page0"] = (0.9 * n((H, T2)) * u).astype(np.float32)
    d["wgs"] = np.exp(0.3 * n((128, S))).astype(np.float32)
    d["base"] = (0.5 * n(H) * u[:, 0]).astype(np.float32)
    d["wy_words"], d["wy_scales"] = pack_weight(n((H, N)) * 1.3 / H ** 0.5 / u, "e4m3")
    d["resid"] = (0.7 * n((N, P))).astype(np.float32)
    d["page1"] = (0.7 * n((N, T2))).astype(np.float32)
    d["wgo"] = np.exp(0.3 * n((128, P))).astype(np.float32)
    d["offs"] = striped(np.random.permutation(T)[:S])
    d["offs2"] = striped(np.random.permutation(T2)[:S])
    d["offs3"] = striped(np.random.permutation(T2)[:P])
    d["offs4"] = striped(np.random.permutation(T2)[:P])
    return d

def reference(tab_words, tab_scales, wa, wd_words, wd_scales, gain, page0, wgs, base, wy_words, wy_scales, resid, page1, wgo, offs, offs2, offs3, offs4):
    v = unpack_weight(tab_words, tab_scales, "e4m3")[:, unstriped(offs)]
    a = mxq(f64(wa), 0, "e4m3").T @ v
    b = unpack_weight(wd_words, wd_scales, "e2m1").T @ v
    h = np.tanh(a) * np.exp(-np.abs(b)) * f64(gain)[:, None]
    page = f64(page0).copy()
    page[:, unstriped(offs2)] = np.tile(f64(wgs), (H // 128, 1)) * h
    x = np.maximum(page[:, unstriped(offs3)], f64(base)[:, None])
    y = (unpack_weight(wy_words, wy_scales, "e4m3").T @ mxq(x, 0, "e4m3")) + f64(resid)
    out = f64(page1).copy()
    out[:, unstriped(offs4)] = np.tile(f64(wgo), (N // 128, 1)) * y
    return out

@@ -1,0 +1,387 @@
+from contextlib import ExitStack
+
+import concourse.mybir as mybir
+from concourse.masks import make_identity
+
+F32 = mybir.dt.float32
+BF16 = mybir.dt.bfloat16
+I32 = mybir.dt.int32
+U32 = mybir.dt.uint32
+U16 = mybir.dt.uint16
+U8 = mybir.dt.uint8
+FP8X4 = mybir.dt.float8_e4m3fn_x4
+FP4X4 = mybir.dt.float4_e2m1fn_x4
+ACT = mybir.ActivationFunctionType
+ALU = mybir.AluOpType
+
+K, T, S, H, T2, N, M = 1536, 2048, 512, 1024, 1024, 768, 512
+P = 128
+KP = K // 512
+RP = H // 512
+SLICES = H // P
+NT = N // P
+HALF = M // 2
+FLOPS = 2 * K * H * S * 2 + 2 * H * N * M
+
+
+def tile_list_trap_spray_scores_kernel(
+    tc, tab_words, tab_scales, wa, wd_words, wd_scales, gain, page0, wgs, base,
+    wy_words, wy_scales, resid, page1, wgo, offs, offs2, offs3, offs4, out,
+):
+    nc = tc.nc
+    with ExitStack() as ctx:
+        keep = ctx.enter_context(tc.tile_pool(name="keep", bufs=1))
+        ring2 = ctx.enter_context(tc.tile_pool(name="ring2", bufs=2))
+        ring3 = ctx.enter_context(tc.tile_pool(name="ring3", bufs=3))
+        pin = ctx.enter_context(tc.tile_pool(name="pin", bufs=1))
+        psum = ctx.enter_context(tc.psum_pool(name="psum", bufs=1))
+
+        def load_list(src, name):
+            t = keep.tile([P, S // 16], U16, name=name)
+            nc.sync.dma_start(t[:], src)
+            return t
+
+        def load_scales(queue, plane, src):
+            passes = src.shape[0]
+            for q in range(4):
+                queue.dma_start(
+                    plane[32 * q : 32 * q + 4, :].bitcast(I32).rearrange("r (a c) -> r a c", a=passes),
+                    src[:, 4 * q : 4 * q + 4, :].bitcast(I32).rearrange("a r c -> r a c"),
+                )
+
+        tab_s = keep.tile([P, KP * T], U8, name="tab_s", align_bytes=64)
+        wd_s = keep.tile([P, KP * H], U8, name="wd_s", align_bytes=64)
+        wy_s = keep.tile([P, RP * N], U8, name="wy_s", align_bytes=64)
+        nc.vector.memset(tab_s[:].bitcast(I32), 0)
+        nc.vector.memset(wd_s[:].bitcast(I32), 0)
+        nc.vector.memset(wy_s[:].bitcast(I32), 0)
+
+        rows = keep.tile([P, P], F32, name="rows")
+        nc.gpsimd.memset(rows[:], 0.0)
+        nc.gpsimd.dma_start(rows[0:SLICES, :], gain.rearrange("(s q) -> s q", q=P))
+        nc.gpsimd.dma_start(rows[SLICES : 2 * SLICES, :], base.rearrange("(s q) -> s q", q=P))
+        ident32 = keep.tile([P, P], F32, name="ident32")
+        make_identity(nc, ident32[:])
+        ident16 = keep.tile([P, P], BF16, name="ident16")
+        make_identity(nc, ident16[:])
+
+        def load_table(a):
+            t = keep.tile([P, T], U32, name="tab_w%d" % a)
+            nc.sync.dma_start(t[:].bitcast(I32), tab_words[a].rearrange("p t i -> p (t i)").bitcast(I32))
+            return t
+
+        def load_wa_pass(dst, a, c0, width):
+            nc.sync.dma_start(dst, wa[512 * a : 512 * (a + 1), c0 : c0 + width].rearrange("(p j) c -> p j c", j=4))
+
+        def load_wa(pool, tag, c0, width):
+            t = pool.tile([P, KP, 4, width], F32, name=tag)
+            for a in range(KP):
+                load_wa_pass(t[:, a], a, c0, width)
+            return t
+
+        def load_wd(name, c0, width):
+            t = keep.tile([P, KP, 2 * width], U8, name=name, align_bytes=64)
+            nc.sync.dma_start(
+                t[:].bitcast(I32), wd_words[:, :, 2 * c0 : 2 * (c0 + width)].bitcast(I32).rearrange("a p c -> p a c")
+            )
+            return t
+
+        def load_rows(src, i, name):
+            t = keep.tile([P, src.shape[1]], F32, name=name)
+            nc.sync.dma_start(t[:], src[P * i : P * (i + 1), :])
+            return t
+
+        list1 = load_list(offs, "list1")
+        list2 = load_list(offs2, "list2")
+        list3 = load_list(offs3, "list3")
+        list4 = load_list(offs4, "list4")
+        tab_w = [load_table(0)]
+        wa_first = []
+        for a in range(KP):
+            t = keep.tile([P, 4, P], F32, name="wa_first%d" % a)
+            load_wa_pass(t[:], a, 0, P)
+            wa_first.append(t)
+        load_scales(nc.scalar, tab_s, tab_scales)
+        tab_w.append(load_table(1))
+        wd_w = {}
+        wa_raw = {}
+        pages = []
+
+        def take_wd(s0, count):
+            t = load_wd("wd_w%d" % s0, P * s0, P * count)
+            for i in range(count):
+                wd_w[s0 + i] = (t, P * i)
+
+        def take_wa(s0, count):
+            t = load_wa(ring2, "wa_raw%d" % count, P * s0, P * count)
+            for i in range(count):
+                wa_raw[s0 + i] = (t, P * i)
+
+        def take_page(s):
+            pages.append(load_rows(page0, s, "page0_%d" % s))
+
+        take_wd(0, 2)
+        tab_w.append(load_table(2))
+        load_scales(nc.sync, wd_s, wd_scales)
+        take_wa(1, 1)
+        wgs_t = load_rows(wgs, 0, "wgs_t")
+        take_page(0)
+        take_wa(2, 1)
+        take_wd(2, 2)
+        take_page(1)
+        take_wa(3, 2)
+        take_page(2)
+        take_wd(4, 4)
+        take_page(3)
+        take_wa(5, 2)
+        take_page(4)
+        take_page(5)
+        take_wa(7, 1)
+        take_page(6)
+        take_page(7)
+        wy_w = keep.tile([P, RP, N], U32, name="wy_w", align_bytes=64)
+        nc.sync.dma_start(wy_w[:].bitcast(I32), wy_words.rearrange("a p c i -> p a (c i)").bitcast(I32))
+        load_scales(nc.sync, wy_s, wy_scales)
+        wgo_t = load_rows(wgo, 0, "wgo_t")
+        res = []
+        outs = []
+        for i in range(NT):
+            res.append(load_rows(resid, i, "res%d" % i))
+            outs.append(load_rows(page1, i, "page1_%d" % i))
+
+        cols_ps = psum.tile([P, P], F32, name="cols_ps", tag="U0")
+        nc.tensor.transpose(cols_ps[:], rows[:], ident32[:])
+        cols = keep.tile([P, 2 * SLICES], F32, name="cols")
+        nc.scalar.copy(cols[:], cols_ps[:, 0 : 2 * SLICES])
+
+        v_s = []
+        v_w = []
+        for a in range(KP):
+            t = keep.tile([P, S], U8, name="v_s%d" % a, align_bytes=64)
+            nc.vector.tensor_copy(t[:], tab_s[:, a * T : (a + 1) * T].indirect(list1[:]))
+            v_s.append(t)
+        for a in range(KP):
+            t = keep.tile([P, S], U32, name="v_w%d" % a, align_bytes=64)
+            nc.vector.tensor_copy(t[:], tab_w[a][:].indirect(list1[:]))
+            v_w.append(t)
+
+        REGION = 3072
+
+        def pinned(kind, s, shape, dtype, region, at):
+            return pin.tile(
+                shape, dtype, name="%s%d" % (kind, s % 2), offset=REGION * (2 * region + s % 2) + at, align_bytes=64
+            )
+
+        wa_b = {}
+        wa_q = {}
+
+        def round_wa(s):
+            wb = pinned("wb", s, [P, KP, P, 4], BF16, 1, 0)
+            if s == 0:
+                for a in range(KP):
+                    nc.scalar.copy(
+                        wb[:, a].rearrange("p (c i) j -> p c j i", i=4),
+                        wa_first[a][:].rearrange("p j (c i) -> p c j i", i=4),
+                    )
+            else:
+                raw, c0 = wa_raw[s]
+                dst = wb[:].rearrange("p a (c i) j -> p a c j i", i=4)
+                src = raw[:, :, :, c0 : c0 + P].rearrange("p a j (c i) -> p a c j i", i=4)
+                if s == 1:
+                    nc.vector.tensor_copy(dst[:, 0:2], src[:, 0:2])
+                    nc.vector.tensor_copy(dst[:, 2], src[:, 2])
+                else:
+                    nc.scalar.copy(dst, src)
+            wa_b[s] = wb
+
+        def quantise_wa(s):
+            codes = ring2.tile([P, KP * P], U32, name="wa_codes", align_bytes=64)
+            scales = pinned("wa_scales", s, [P, KP * P], U8, 0, 0)
+            flat = wa_b[s][:].rearrange("p a c j -> p (a c j)")
+            spans = [(0, P), (P, 2 * P), (2 * P, 3 * P)] if s == 0 else [(0, 2 * P), (2 * P, 3 * P)]
+            for lo, hi in spans:
+                nc.vector.quantize_mx(
+                    out=codes[:, lo:hi].bitcast(FP8X4), scales=scales[:, lo:hi], in_=flat[:, 4 * lo : 4 * hi]
+                )
+            wa_q[s] = (codes, scales)
+
+        states = {}
+
+        def make_states(s):
+            codes, scales = wa_q[s]
+            wd_t, c0 = wd_w[s]
+            gain_s = cols[:, s : s + 1]
+            if s > 0:
+                factor = pinned("factor", s, [P, S], F32, 1, 1024)
+                nc.gpsimd.tensor_scalar(factor[:], wgs_t[:], gain_s, 0.0, ALU.mult, ALU.add)
+            b_ps = psum.tile([P, S], F32, name="b_ps", tag="B%d" % (s % 2))
+            a_ps = psum.tile([P, S], F32, name="a_ps", tag="A%d" % (s % 2))
+            for a in range(KP):
+                nc.tensor.matmul_mx(
+                    out=b_ps[:],
+                    lhsT=wd_t[:, a, 2 * c0 : 2 * (c0 + P)].bitcast(FP4X4),
+                    lhsT_scale=wd_s[:, a * H + P * s : a * H + P * (s + 1)],
+                    rhs=v_w[a][:].bitcast(FP8X4),
+                    rhs_scale=v_s[a][:],
+                    start=(a == 0),
+                    stop=(a == KP - 1),
+                )
+            for a in range(KP):
+                nc.tensor.matmul_mx(
+                    out=a_ps[:],
+                    lhsT=codes[:, P * a : P * (a + 1)].bitcast(FP8X4),
+                    lhsT_scale=scales[:, P * a : P * (a + 1)],
+                    rhs=v_w[a][:].bitcast(FP8X4),
+                    rhs_scale=v_s[a][:],
+                    start=(a == 0),
+                    stop=(a == KP - 1),
+                )
+            damp = ring2.tile([P, S], F32, name="damp")
+            resp = ring2.tile([P, S], F32, name="resp")
+            weight = ring2.tile([P, S], F32, name="weight")
+            nc.scalar.activation(damp[:], b_ps[:], ACT.Abs)
+            nc.scalar.activation(damp[:], damp[:], ACT.Exp, scale=-1.0)
+            nc.scalar.activation(resp[:], a_ps[:], ACT.Tanh)
+            if s == SLICES - 1:
+                h = keep.tile([P, S], F32, name="h_last", tag="hold1")
+            else:
+                h = pinned("h", s, [P, S], F32, 0, 0)
+            if s == 0:
+                nc.vector.tensor_tensor(weight[:], damp[:], wgs_t[:], ALU.mult)
+                nc.vector.scalar_tensor_tensor(h[:], resp[:], gain_s, weight[:], ALU.mult, ALU.mult)
+            else:
+                nc.gpsimd.tensor_tensor(weight[:], damp[:], factor[:], ALU.mult)
+                nc.gpsimd.tensor_tensor(h[:], resp[:], weight[:], ALU.mult)
+            states[s] = h
+
+        def put_states(s):
+            nc.vector.tensor_copy(pages[s][:].indirect(list2[:]), states[s][:])
+
+        def recall(s, picked, lo, hi):
+            nc.vector.tensor_copy(picked, pages[s][:].indirect(list3[:, lo // 16 : hi // 16]))
+
+        def bound(s, x, picked):
+            nc.gpsimd.tensor_scalar(x, picked, cols[:, SLICES + s : SLICES + s + 1], 0.0, ALU.max, ALU.add)
+
+        def turn(s, x, x_t, blocks, tag):
+            ps = psum.tile([P, blocks, P], BF16, name="turn_ps", tag=tag)
+            for mb in range(blocks):
+                nc.tensor.transpose(ps[:, mb, :], x[:, P * mb : P * (mb + 1)], ident16[:])
+            sl = s % 4
+            nc.scalar.copy(x_t[:, :, P * sl : P * (sl + 1)], ps[:])
+
+        def turn_back(x_t, mb0, grouped, tag):
+            words = x_t[:].bitcast(F32)
+            ps = psum.tile([P, 2, 2, P], F32, name="back_ps", tag=tag)
+            for mb in range(2):
+                for u in range(2):
+                    nc.tensor.transpose(ps[:, mb, u, :], words[:, mb0 + mb, u : 256 : 2], ident32[:])
+            nc.scalar.copy(
+                grouped.bitcast(F32).rearrange("p (b m u) -> p b m u", b=2, u=2),
+                ps[:].rearrange("p b u m -> p b m u"),
+            )
+
+        x_t0 = keep.tile([P, 4, 512], BF16, name="x_t0")
+        x_t1 = [keep.tile([P, 2, 512], BF16, name="x_t1%d" % i) for i in range(2)]
+        x0_w = keep.tile([P, M], U32, name="x0_w", align_bytes=64)
+        x0_s = keep.tile([P, M], U8, name="x0_s", align_bytes=64)
+        x1_w = [keep.tile([P, HALF], U32, name="x1_w%d" % i, align_bytes=64) for i in range(2)]
+        x1_s = [keep.tile([P, HALF], U8, name="x1_s%d" % i, align_bytes=64) for i in range(2)]
+
+        round_wa(0)
+        quantise_wa(0)
+        round_wa(1)
+        quantise_wa(1)
+        make_states(0)
+        make_states(1)
+        round_wa(2)
+        for s in range(SLICES):
+            put_states(s)
+            r = s - 1
+            width = M if r < 4 else HALF
+            if r >= 0:
+                picked = pinned("picked", s, [P, M], F32, 0, 1024)
+                recall(r, picked[:, 0:width], 0, width)
+            if s + 2 < SLICES:
+                quantise_wa(s + 2)
+            if r >= 0:
+                x = pinned("x", s, [P, M], BF16, 1, 0)
+                bound(r, x[:, 0:width], picked[:, 0:width])
+            if s + 2 < SLICES:
+                make_states(s + 2)
+            if r >= 0:
+                turn(r, x, x_t0 if r < 4 else x_t1[0], width // P, "A%d" % (s % 2))
+            if r == 3:
+                grouped = keep.tile([P, 4 * M], BF16, name="grouped0", align_bytes=64)
+                for i in range(2):
+                    turn_back(x_t0, 2 * i, grouped[:, 4 * HALF * i : 4 * HALF * (i + 1)], "U%d" % i)
+                nc.vector.quantize_mx(out=x0_w[:].bitcast(FP8X4), scales=x0_s[:], in_=grouped[:])
+            if s + 3 < SLICES:
+                round_wa(s + 3)
+
+        def recall_half(s, picked, hf, tag):
+            recall(s, picked, HALF * hf, HALF * (hf + 1))
+            x = ring3.tile([P, HALF], BF16, name="x_half")
+            bound(s, x[:], picked)
+            turn(s, x, x_t1[hf], 2, tag)
+
+        def quantise_half(i, tag):
+            grouped = keep.tile([P, 4 * HALF], BF16, name="grouped1", tag=tag, align_bytes=64)
+            turn_back(x_t1[i], 0, grouped[:], "U%d" % i)
+            nc.vector.quantize_mx(out=x1_w[i][:].bitcast(FP8X4), scales=x1_s[i][:], in_=grouped[:])
+
+        late = keep.tile([P, 4, HALF], F32, name="late", tag="hold1")
+        recall_half(7, late[:, 0, :], 0, "B0")
+        quantise_half(0, "hold2")
+        for s in range(4, 7):
+            recall_half(s, late[:, s - 3, :], 1, ["B1", "A0", "A1"][s - 4])
+        last = keep.tile([P, HALF], F32, name="last", tag="hold2", align_bytes=64)
+        recall_half(7, last[:], 1, "B0")
+
+        banks = ["Y0", "Y1", "B1", "A0"]
+
+        def score(turn_no, i, halves):
+            lo, hi = HALF * halves[0], HALF * (halves[-1] + 1)
+            ps = psum.tile([P, M], F32, name="y_ps", tag=banks[turn_no % 4])
+            for hf in halves:
+                cols_h = slice(HALF * hf, HALF * (hf + 1))
+                nc.tensor.matmul_mx(
+                    out=ps[:, cols_h],
+                    lhsT=wy_w[:, 0, P * i : P * (i + 1)].bitcast(FP8X4),
+                    lhsT_scale=wy_s[:, P * i : P * (i + 1)],
+                    rhs=x0_w[:, cols_h].bitcast(FP8X4),
+                    rhs_scale=x0_s[:, cols_h],
+                    start=True,
+                    stop=False,
+                )
+                nc.tensor.matmul_mx(
+                    out=ps[:, cols_h],
+                    lhsT=wy_w[:, 1, P * i : P * (i + 1)].bitcast(FP8X4),
+                    lhsT_scale=wy_s[:, N + P * i : N + P * (i + 1)],
+                    rhs=x1_w[hf][:].bitcast(FP8X4),
+                    rhs_scale=x1_s[hf][:],
+                    start=False,
+                    stop=True,
+                )
+            y = ring2.tile([P, M], F32, name="y")
+            scored = ring3.tile([P, M], F32, name="scored")
+            if turn_no == 0:
+                nc.vector.tensor_tensor(y[:, lo:hi], ps[:, lo:hi], res[i][:, lo:hi], ALU.add)
+                nc.vector.tensor_tensor(scored[:, lo:hi], y[:, lo:hi], wgo_t[:, lo:hi], ALU.mult)
+            else:
+                nc.scalar.copy(y[:, lo:hi], ps[:, lo:hi])
+                nc.gpsimd.tensor_tensor(y[:, lo:hi], y[:, lo:hi], res[i][:, lo:hi], ALU.add)
+                nc.gpsimd.tensor_tensor(scored[:, lo:hi], y[:, lo:hi], wgo_t[:, lo:hi], ALU.mult)
+            nc.vector.tensor_copy(outs[i][:].indirect(list4[:, lo // 16 : hi // 16]), scored[:, lo:hi])
+            if hi == M:
+                nc.sync.dma_start(out[P * i : P * (i + 1), :], outs[i][:])
+
+        score(0, 0, [0])
+        score(1, 1, [0])
+        quantise_half(1, "hold3")
+        score(2, 2, [0])
+        score(3, 3, [0])
+        for i in range(4):
+            score(4 + i, i, [1])
+        for i in range(4, NT):
+            score(4 + i, i, [0, 1])

@@ -21,6 +21,7 @@ RP = H // 512
 SLICES = H // P
 NT = N // P
 HALF = M // 2
+PASS_ORDER = (0, 1)
 FLOPS = 2 * K * H * S * 2 + 2 * H * N * M
 
 
@@ -52,18 +53,16 @@ def tile_list_trap_spray_scores_kernel(
         tab_s = keep.tile([P, KP * T], U8, name="tab_s", align_bytes=64)
         wd_s = keep.tile([P, KP * H], U8, name="wd_s", align_bytes=64)
         wy_s = keep.tile([P, RP * N], U8, name="wy_s", align_bytes=64)
+        rows = keep.tile([P, P], F32, name="rows")
+        nc.vector.memset(rows[:], 0.0)
         nc.vector.memset(tab_s[:].bitcast(I32), 0)
         nc.vector.memset(wd_s[:].bitcast(I32), 0)
         nc.vector.memset(wy_s[:].bitcast(I32), 0)
 
-        rows = keep.tile([P, P], F32, name="rows")
-        nc.gpsimd.memset(rows[:], 0.0)
-        nc.gpsimd.dma_start(rows[0:SLICES, :], gain.rearrange("(s q) -> s q", q=P))
-        nc.gpsimd.dma_start(rows[SLICES : 2 * SLICES, :], base.rearrange("(s q) -> s q", q=P))
         ident32 = keep.tile([P, P], F32, name="ident32")
         make_identity(nc, ident32[:])
         ident16 = keep.tile([P, P], BF16, name="ident16")
-        make_identity(nc, ident16[:])
+        nc.scalar.copy(ident16[:], ident32[:])
 
         def load_table(a):
             t = keep.tile([P, T], U32, name="tab_w%d" % a)
@@ -91,18 +90,6 @@ def tile_list_trap_spray_scores_kernel(
             nc.sync.dma_start(t[:], src[P * i : P * (i + 1), :])
             return t
 
-        list1 = load_list(offs, "list1")
-        list2 = load_list(offs2, "list2")
-        list3 = load_list(offs3, "list3")
-        list4 = load_list(offs4, "list4")
-        tab_w = [load_table(0)]
-        wa_first = []
-        for a in range(KP):
-            t = keep.tile([P, 4, P], F32, name="wa_first%d" % a)
-            load_wa_pass(t[:], a, 0, P)
-            wa_first.append(t)
-        load_scales(nc.scalar, tab_s, tab_scales)
-        tab_w.append(load_table(1))
         wd_w = {}
         wa_raw = {}
         pages = []
@@ -113,30 +100,41 @@ def tile_list_trap_spray_scores_kernel(
                 wd_w[s0 + i] = (t, P * i)
 
         def take_wa(s0, count):
-            t = load_wa(ring2, "wa_raw%d" % count, P * s0, P * count)
+            t = load_wa(keep, "wa_raw%d" % s0, P * s0, P * count)
             for i in range(count):
                 wa_raw[s0 + i] = (t, P * i)
 
         def take_page(s):
             pages.append(load_rows(page0, s, "page0_%d" % s))
 
-        take_wd(0, 2)
-        tab_w.append(load_table(2))
+        list1 = load_list(offs, "list1")
+        list2 = load_list(offs2, "list2")
+        list3 = load_list(offs3, "list3")
+        list4 = load_list(offs4, "list4")
+        tab_w = [load_table(0)]
+        nc.sync.dma_start(rows[0:SLICES, :], gain.rearrange("(s q) -> s q", q=P))
+        nc.sync.dma_start(rows[SLICES : 2 * SLICES, :], base.rearrange("(s q) -> s q", q=P))
+        take_wd(0, 4)
+        load_scales(nc.sync, tab_s, tab_scales)
+        tab_w.append(load_table(1))
         load_scales(nc.sync, wd_s, wd_scales)
-        take_wa(1, 1)
+        tab_w.append(load_table(2))
+        wa_first = []
+        for a in range(KP):
+            t = keep.tile([P, 4, 2 * P], F32, name="wa_first%d" % a)
+            load_wa_pass(t[:], a, 0, 2 * P)
+            wa_first.append(t)
         wgs_t = load_rows(wgs, 0, "wgs_t")
         take_page(0)
-        take_wa(2, 1)
-        take_wd(2, 2)
+        take_wa(2, 2)
         take_page(1)
-        take_wa(3, 2)
         take_page(2)
         take_wd(4, 4)
+        take_wa(4, 2)
         take_page(3)
-        take_wa(5, 2)
         take_page(4)
+        take_wa(6, 2)
         take_page(5)
-        take_wa(7, 1)
         take_page(6)
         take_page(7)
         wy_w = keep.tile([P, RP, N], U32, name="wy_w", align_bytes=64)
@@ -147,6 +145,7 @@ def tile_list_trap_spray_scores_kernel(
         outs = []
         for i in range(NT):
             res.append(load_rows(resid, i, "res%d" % i))
+        for i in range(NT):
             outs.append(load_rows(page1, i, "page1_%d" % i))
 
         cols_ps = psum.tile([P, P], F32, name="cols_ps", tag="U0")
@@ -165,57 +164,51 @@ def tile_list_trap_spray_scores_kernel(
             nc.vector.tensor_copy(t[:], tab_w[a][:].indirect(list1[:]))
             v_w.append(t)
 
-        REGION = 3072
+        def pinned(kind, s, at, shape, dtype):
+            return pin.tile(shape, dtype, name="%s%d" % (kind, s % 2), offset=3072 * (s % 2) + at, align_bytes=64)
 
-        def pinned(kind, s, shape, dtype, region, at):
-            return pin.tile(
-                shape, dtype, name="%s%d" % (kind, s % 2), offset=REGION * (2 * region + s % 2) + at, align_bytes=64
-            )
+        def held(kind, at, shape, dtype):
+            return pin.tile(shape, dtype, name=kind, offset=6144 + at, align_bytes=64)
 
         wa_b = {}
         wa_q = {}
 
         def round_wa(s):
-            wb = pinned("wb", s, [P, KP, P, 4], BF16, 1, 0)
-            if s == 0:
+            lead = pinned("wb_lead", s, 512, [P, 2, P, 4], BF16)
+            rest = ring2.tile([P, P, 4], BF16, name="wb_rest", align_bytes=64)
+            if s < 2:
                 for a in range(KP):
-                    nc.scalar.copy(
-                        wb[:, a].rearrange("p (c i) j -> p c j i", i=4),
-                        wa_first[a][:].rearrange("p j (c i) -> p c j i", i=4),
-                    )
+                    dst = (lead[:, a] if a < 2 else rest[:]).rearrange("p (c i) j -> p c j i", i=4)
+                    src = wa_first[a][:, :, P * s : P * (s + 1)].rearrange("p j (c i) -> p c j i", i=4)
+                    nc.vector.tensor_copy(dst, src)
             else:
                 raw, c0 = wa_raw[s]
-                dst = wb[:].rearrange("p a (c i) j -> p a c j i", i=4)
                 src = raw[:, :, :, c0 : c0 + P].rearrange("p a j (c i) -> p a c j i", i=4)
-                if s == 1:
-                    nc.vector.tensor_copy(dst[:, 0:2], src[:, 0:2])
-                    nc.vector.tensor_copy(dst[:, 2], src[:, 2])
-                else:
-                    nc.scalar.copy(dst, src)
-            wa_b[s] = wb
+                nc.scalar.copy(rest[:].rearrange("p (c i) j -> p c j i", i=4), src[:, 2])
+                nc.scalar.copy(lead[:].rearrange("p a (c i) j -> p a c j i", i=4), src[:, 0:2])
+            wa_b[s] = (lead, rest)
 
         def quantise_wa(s):
             codes = ring2.tile([P, KP * P], U32, name="wa_codes", align_bytes=64)
-            scales = pinned("wa_scales", s, [P, KP * P], U8, 0, 0)
-            flat = wa_b[s][:].rearrange("p a c j -> p (a c j)")
-            spans = [(0, P), (P, 2 * P), (2 * P, 3 * P)] if s == 0 else [(0, 2 * P), (2 * P, 3 * P)]
-            for lo, hi in spans:
-                nc.vector.quantize_mx(
-                    out=codes[:, lo:hi].bitcast(FP8X4), scales=scales[:, lo:hi], in_=flat[:, 4 * lo : 4 * hi]
-                )
+            scales = ring2.tile([P, KP * P], U8, name="wa_scales", align_bytes=64)
+            lead, rest = wa_b[s]
+            parts = [
+                (0, 2 * P, lead[:].rearrange("p a c j -> p (a c j)")),
+                (2 * P, 3 * P, rest[:].rearrange("p c j -> p (c j)")),
+            ]
+            if s == 0:
+                parts[0:1] = [(P * a, P * (a + 1), lead[:, a].rearrange("p c j -> p (c j)")) for a in range(2)]
+            for lo, hi, src in parts if s < 2 else reversed(parts):
+                nc.vector.quantize_mx(out=codes[:, lo:hi].bitcast(FP8X4), scales=scales[:, lo:hi], in_=src)
             wa_q[s] = (codes, scales)
 
+        damps = {}
+        resps = {}
         states = {}
 
-        def make_states(s):
-            codes, scales = wa_q[s]
+        def make_damping(s):
             wd_t, c0 = wd_w[s]
-            gain_s = cols[:, s : s + 1]
-            if s > 0:
-                factor = pinned("factor", s, [P, S], F32, 1, 1024)
-                nc.gpsimd.tensor_scalar(factor[:], wgs_t[:], gain_s, 0.0, ALU.mult, ALU.add)
-            b_ps = psum.tile([P, S], F32, name="b_ps", tag="B%d" % (s % 2))
-            a_ps = psum.tile([P, S], F32, name="a_ps", tag="A%d" % (s % 2))
+            b_ps = psum.tile([P, S], F32, name="b_ps", tag=("A%d" if s in (2, 3) else "B%d") % (s % 2))
             for a in range(KP):
                 nc.tensor.matmul_mx(
                     out=b_ps[:],
@@ -226,42 +219,54 @@ def tile_list_trap_spray_scores_kernel(
                     start=(a == 0),
                     stop=(a == KP - 1),
                 )
-            for a in range(KP):
-                nc.tensor.matmul_mx(
-                    out=a_ps[:],
-                    lhsT=codes[:, P * a : P * (a + 1)].bitcast(FP8X4),
-                    lhsT_scale=scales[:, P * a : P * (a + 1)],
-                    rhs=v_w[a][:].bitcast(FP8X4),
-                    rhs_scale=v_s[a][:],
-                    start=(a == 0),
-                    stop=(a == KP - 1),
-                )
             damp = ring2.tile([P, S], F32, name="damp")
-            resp = ring2.tile([P, S], F32, name="resp")
-            weight = ring2.tile([P, S], F32, name="weight")
             nc.scalar.activation(damp[:], b_ps[:], ACT.Abs)
             nc.scalar.activation(damp[:], damp[:], ACT.Exp, scale=-1.0)
-            nc.scalar.activation(resp[:], a_ps[:], ACT.Tanh)
+            damps[s] = damp
+
+        def spans(s):
+            return [(0, S // 2), (S // 2, S)] if s == 0 else [(0, S)]
+
+        def make_response(s):
+            codes, scales = wa_q[s]
+            resp = ring2.tile([P, S], F32, name="resp")
+            for lo, hi in spans(s):
+                a_ps = psum.tile([P, hi - lo], F32, name="a_ps", tag="U1" if lo else "A%d" % (s % 2))
+                for a in range(KP):
+                    nc.tensor.matmul_mx(
+                        out=a_ps[:],
+                        lhsT=codes[:, P * a : P * (a + 1)].bitcast(FP8X4),
+                        lhsT_scale=scales[:, P * a : P * (a + 1)],
+                        rhs=v_w[a][:, lo:hi].bitcast(FP8X4),
+                        rhs_scale=v_s[a][:, lo:hi],
+                        start=(a == 0),
+                        stop=(a == KP - 1),
+                    )
+                nc.scalar.activation(resp[:, lo:hi], a_ps[:], ACT.Tanh)
+            resps[s] = resp
+
+        def make_states(s):
             if s == SLICES - 1:
-                h = keep.tile([P, S], F32, name="h_last", tag="hold1")
+                h = held("h_last", 0, [P, S], F32)
             else:
-                h = pinned("h", s, [P, S], F32, 0, 0)
-            if s == 0:
-                nc.vector.tensor_tensor(weight[:], damp[:], wgs_t[:], ALU.mult)
-                nc.vector.scalar_tensor_tensor(h[:], resp[:], gain_s, weight[:], ALU.mult, ALU.mult)
-            else:
-                nc.gpsimd.tensor_tensor(weight[:], damp[:], factor[:], ALU.mult)
-                nc.gpsimd.tensor_tensor(h[:], resp[:], weight[:], ALU.mult)
+                h = pinned("h", s + 1, 0, [P, S], F32)
+            for lo, hi in spans(s):
+                nc.vector.scalar_tensor_tensor(
+                    h[:, lo:hi], resps[s][:, lo:hi], cols[:, s : s + 1], damps[s][:, lo:hi], ALU.mult, ALU.mult
+                )
             states[s] = h
 
         def put_states(s):
-            nc.vector.tensor_copy(pages[s][:].indirect(list2[:]), states[s][:])
+            for lo, hi in spans(s):
+                nc.vector.tensor_tensor(
+                    pages[s][:].indirect(list2[:, lo // 16 : hi // 16]), states[s][:, lo:hi], wgs_t[:, lo:hi], ALU.mult
+                )
 
         def recall(s, picked, lo, hi):
             nc.vector.tensor_copy(picked, pages[s][:].indirect(list3[:, lo // 16 : hi // 16]))
 
         def bound(s, x, picked):
-            nc.gpsimd.tensor_scalar(x, picked, cols[:, SLICES + s : SLICES + s + 1], 0.0, ALU.max, ALU.add)
+            nc.vector.tensor_scalar(x, picked, cols[:, SLICES + s : SLICES + s + 1], None, ALU.max)
 
         def turn(s, x, x_t, blocks, tag):
             ps = psum.tile([P, blocks, P], BF16, name="turn_ps", tag=tag)
@@ -281,43 +286,59 @@ def tile_list_trap_spray_scores_kernel(
                 ps[:].rearrange("p b u m -> p b m u"),
             )
 
+        grouped0 = keep.tile([P, 4 * M], BF16, name="grouped0", align_bytes=64)
         x_t0 = keep.tile([P, 4, 512], BF16, name="x_t0")
         x_t1 = [keep.tile([P, 2, 512], BF16, name="x_t1%d" % i) for i in range(2)]
         x0_w = keep.tile([P, M], U32, name="x0_w", align_bytes=64)
-        x0_s = keep.tile([P, M], U8, name="x0_s", align_bytes=64)
         x1_w = [keep.tile([P, HALF], U32, name="x1_w%d" % i, align_bytes=64) for i in range(2)]
         x1_s = [keep.tile([P, HALF], U8, name="x1_s%d" % i, align_bytes=64) for i in range(2)]
 
+        make_damping(0)
         round_wa(0)
         quantise_wa(0)
+        make_response(0)
         round_wa(1)
         quantise_wa(1)
         make_states(0)
-        make_states(1)
+        make_damping(1)
+        make_response(1)
         round_wa(2)
-        for s in range(SLICES):
+        for s in range(SLICES - 1):
             put_states(s)
-            r = s - 1
-            width = M if r < 4 else HALF
-            if r >= 0:
-                picked = pinned("picked", s, [P, M], F32, 0, 1024)
-                recall(r, picked[:, 0:width], 0, width)
+            width = M if s < 4 else HALF
+            picked = ring2.tile([P, M], F32, name="picked")
+            recall(s, picked[:, 0:width], 0, width)
             if s + 2 < SLICES:
                 quantise_wa(s + 2)
-            if r >= 0:
-                x = pinned("x", s, [P, M], BF16, 1, 0)
-                bound(r, x[:, 0:width], picked[:, 0:width])
+            make_states(s + 1)
+            x = pinned("x", s, 2048, [P, M], BF16)
+            bound(s, x[:, 0:width], picked[:, 0:width])
             if s + 2 < SLICES:
-                make_states(s + 2)
-            if r >= 0:
-                turn(r, x, x_t0 if r < 4 else x_t1[0], width // P, "A%d" % (s % 2))
-            if r == 3:
-                grouped = keep.tile([P, 4 * M], BF16, name="grouped0", align_bytes=64)
-                for i in range(2):
-                    turn_back(x_t0, 2 * i, grouped[:, 4 * HALF * i : 4 * HALF * (i + 1)], "U%d" % i)
-                nc.vector.quantize_mx(out=x0_w[:].bitcast(FP8X4), scales=x0_s[:], in_=grouped[:])
+                make_damping(s + 2)
+                make_response(s + 2)
             if s + 3 < SLICES:
                 round_wa(s + 3)
+            turn(s, x, x_t0 if s < 4 else x_t1[0], width // P, "Y%d" % (s % 2))
+            if s == 3:
+                for i in range(2):
+                    turn_back(x_t0, 2 * i, grouped0[:, 4 * HALF * i : 4 * HALF * (i + 1)], "U%d" % i)
+        put_states(SLICES - 1)
+
+        pieces = [([0], 2 * P, 4 * P), ([1], 2 * P, 4 * P), ([2, 3], 0, 2 * P), ([2], 2 * P, 4 * P), ([3], 2 * P, 4 * P)]
+
+        def place(mb, i):
+            for k, (blocks, n0, count) in enumerate(pieces):
+                if mb in blocks and n0 <= P * i < n0 + count:
+                    return k, count * blocks.index(mb) + P * i - n0
+
+        res_t = keep.tile([P, len(pieces), 4 * P], F32, name="res_t", tag="wa_raw2")
+        for k, (blocks, n0, count) in enumerate(pieces):
+            ps = psum.tile([P, 4 * P], F32, name="rt_ps", tag="U%d" % (k % 2))
+            for mb in blocks:
+                for i in range(n0 // P, (n0 + count) // P):
+                    at = place(mb, i)[1]
+                    nc.tensor.transpose(ps[:, at : at + P], res[i][:, P * mb : P * (mb + 1)], ident32[:])
+            nc.scalar.copy(res_t[:, k, :], ps[:])
 
         def recall_half(s, picked, hf, tag):
             recall(s, picked, HALF * hf, HALF * (hf + 1))
@@ -330,58 +351,83 @@ def tile_list_trap_spray_scores_kernel(
             turn_back(x_t1[i], 0, grouped[:], "U%d" % i)
             nc.vector.quantize_mx(out=x1_w[i][:].bitcast(FP8X4), scales=x1_s[i][:], in_=grouped[:])
 
-        late = keep.tile([P, 4, HALF], F32, name="late", tag="hold1")
+        late = held("late", 1024, [P, 4, HALF], F32)
         recall_half(7, late[:, 0, :], 0, "B0")
+        x0_s = held("x0_s", 0, [P, M], U8)
+        nc.vector.quantize_mx(out=x0_w[:].bitcast(FP8X4), scales=x0_s[:], in_=grouped0[:])
         quantise_half(0, "hold2")
         for s in range(4, 7):
-            recall_half(s, late[:, s - 3, :], 1, ["B1", "A0", "A1"][s - 4])
+            recall_half(s, late[:, s - 3, :], 1, "U0")
         last = keep.tile([P, HALF], F32, name="last", tag="hold2", align_bytes=64)
         recall_half(7, last[:], 1, "B0")
 
-        banks = ["Y0", "Y1", "B1", "A0"]
+        y_t = keep.tile([P, len(pieces), 4 * P], F32, name="y_t", tag="wa_raw4")
 
-        def score(turn_no, i, halves):
-            lo, hi = HALF * halves[0], HALF * (halves[-1] + 1)
-            ps = psum.tile([P, M], F32, name="y_ps", tag=banks[turn_no % 4])
-            for hf in halves:
-                cols_h = slice(HALF * hf, HALF * (hf + 1))
-                nc.tensor.matmul_mx(
-                    out=ps[:, cols_h],
-                    lhsT=wy_w[:, 0, P * i : P * (i + 1)].bitcast(FP8X4),
-                    lhsT_scale=wy_s[:, P * i : P * (i + 1)],
-                    rhs=x0_w[:, cols_h].bitcast(FP8X4),
-                    rhs_scale=x0_s[:, cols_h],
-                    start=True,
-                    stop=False,
-                )
-                nc.tensor.matmul_mx(
-                    out=ps[:, cols_h],
-                    lhsT=wy_w[:, 1, P * i : P * (i + 1)].bitcast(FP8X4),
-                    lhsT_scale=wy_s[:, N + P * i : N + P * (i + 1)],
-                    rhs=x1_w[hf][:].bitcast(FP8X4),
-                    rhs_scale=x1_s[hf][:],
-                    start=False,
-                    stop=True,
-                )
-            y = ring2.tile([P, M], F32, name="y")
-            scored = ring3.tile([P, M], F32, name="scored")
-            if turn_no == 0:
-                nc.vector.tensor_tensor(y[:, lo:hi], ps[:, lo:hi], res[i][:, lo:hi], ALU.add)
-                nc.vector.tensor_tensor(scored[:, lo:hi], y[:, lo:hi], wgo_t[:, lo:hi], ALU.mult)
-            else:
-                nc.scalar.copy(y[:, lo:hi], ps[:, lo:hi])
-                nc.gpsimd.tensor_tensor(y[:, lo:hi], y[:, lo:hi], res[i][:, lo:hi], ALU.add)
-                nc.gpsimd.tensor_tensor(scored[:, lo:hi], y[:, lo:hi], wgo_t[:, lo:hi], ALU.mult)
-            nc.vector.tensor_copy(outs[i][:].indirect(list4[:, lo // 16 : hi // 16]), scored[:, lo:hi])
-            if hi == M:
+        def x_operand(a, mb):
+            if a == 0:
+                return x0_w[:, P * mb : P * (mb + 1)], x0_s[:, P * mb : P * (mb + 1)]
+            cols_m = slice(P * (mb % 2), P * (mb % 2 + 1))
+            return x1_w[mb // 2][:, cols_m], x1_s[mb // 2][:, cols_m]
+
+        def product_turned(k, tag):
+            blocks, n0, count = pieces[k]
+            ps = psum.tile([P, 4 * P], F32, name="yt_ps", tag=tag)
+            for j, mb in enumerate(blocks):
+                for a in PASS_ORDER:
+                    words, scales = x_operand(a, mb)
+                    nc.tensor.matmul_mx(
+                        out=ps[:, count * j : count * (j + 1)],
+                        lhsT=words.bitcast(FP8X4),
+                        lhsT_scale=scales,
+                        rhs=wy_w[:, a, n0 : n0 + count].bitcast(FP8X4),
+                        rhs_scale=wy_s[:, N * a + n0 : N * a + n0 + count],
+                        start=(a == PASS_ORDER[0]),
+                        stop=(a == PASS_ORDER[1]),
+                    )
+            nc.scalar.copy(y_t[:, k, :], ps[:])
+
+        def put_scores(i, hf, y):
+            lo, hi = HALF * hf, HALF * (hf + 1)
+            nc.vector.tensor_tensor(outs[i][:].indirect(list4[:, lo // 16 : hi // 16]), y[:], wgo_t[:, lo:hi], ALU.mult)
+            if hf == 1:
                 nc.sync.dma_start(out[P * i : P * (i + 1), :], outs[i][:])
 
-        score(0, 0, [0])
-        score(1, 1, [0])
+        def score_direct(i, tag):
+            ps = psum.tile([P, HALF], F32, name="y_ps", tag=tag)
+            for a in range(RP):
+                words, scales = (x0_w[:, 0:HALF], x0_s[:, 0:HALF]) if a == 0 else (x1_w[0][:], x1_s[0][:])
+                nc.tensor.matmul_mx(
+                    out=ps[:],
+                    lhsT=wy_w[:, a, P * i : P * (i + 1)].bitcast(FP8X4),
+                    lhsT_scale=wy_s[:, N * a + P * i : N * a + P * (i + 1)],
+                    rhs=words.bitcast(FP8X4),
+                    rhs_scale=scales,
+                    start=(a == 0),
+                    stop=(a == RP - 1),
+                )
+            y = ring3.tile([P, HALF], F32, name="y")
+            nc.vector.tensor_tensor(y[:], ps[:], res[i][:, 0:HALF], ALU.add)
+            put_scores(i, 0, y)
+
+        def score_turned(i, hf, tag):
+            ps = psum.tile([P, 2, P], F32, name="sum_ps", tag=tag)
+            for j in range(2):
+                k, at = place(2 * hf + j, i)
+                nc.tensor.matmul(ps[:, j, :], res_t[:, k, at : at + P], ident32[:], start=True, stop=False, is_transpose=True)
+                nc.tensor.matmul(ps[:, j, :], y_t[:, k, at : at + P], ident32[:], start=False, stop=True, is_transpose=True)
+            y = ring3.tile([P, HALF], F32, name="y")
+            nc.scalar.copy(y[:], ps[:].rearrange("p j m -> p (j m)"))
+            put_scores(i, hf, y)
+
+        score_direct(0, "Y0")
+        score_direct(1, "Y1")
+        product_turned(0, "A0")
+        product_turned(1, "A1")
         quantise_half(1, "hold3")
-        score(2, 2, [0])
-        score(3, 3, [0])
-        for i in range(4):
-            score(4 + i, i, [1])
-        for i in range(4, NT):
-            score(4 + i, i, [0, 1])
+        for i in range(2, NT):
+            score_turned(i, 0, "Y%d" % (i % 2))
+        product_turned(2, "B1")
+        product_turned(3, "A0")
+        product_turned(4, "A1")
+        for i in range(NT):
+            score_turned(i, 1, ["B0", "U0"][i % 2])

@@ -42,21 +42,18 @@ def tile_list_trap_spray_scores_kernel(
             nc.sync.dma_start(t[:], src)
             return t
 
-        def load_scales(queue, plane, src):
+        def load_scales(plane, src):
             passes = src.shape[0]
             for q in range(4):
-                queue.dma_start(
+                nc.sync.dma_start(
                     plane[32 * q : 32 * q + 4, :].bitcast(I32).rearrange("r (a c) -> r a c", a=passes),
                     src[:, 4 * q : 4 * q + 4, :].bitcast(I32).rearrange("a r c -> r a c"),
                 )
 
         tab_s = keep.tile([P, KP * T], U8, name="tab_s", align_bytes=64)
-        wd_s = keep.tile([P, KP * H], U8, name="wd_s", align_bytes=64)
         wy_s = keep.tile([P, RP * N], U8, name="wy_s", align_bytes=64)
-        rows = keep.tile([P, P], F32, name="rows")
-        nc.vector.memset(rows[:], 0.0)
-        nc.vector.memset(tab_s[:].bitcast(I32), 0)
-        nc.vector.memset(wd_s[:].bitcast(I32), 0)
+        nc.gpsimd.memset(tab_s[:, 0 : KP * T // 2].bitcast(I32), 0)
+        nc.vector.memset(tab_s[:, KP * T // 2 : KP * T].bitcast(I32), 0)
         nc.vector.memset(wy_s[:].bitcast(I32), 0)
 
         ident32 = keep.tile([P, P], F32, name="ident32")
@@ -64,9 +61,12 @@ def tile_list_trap_spray_scores_kernel(
         ident16 = keep.tile([P, P], BF16, name="ident16")
         nc.scalar.copy(ident16[:], ident32[:])
 
-        def load_table(a):
+        def load_table(a, parts=1):
             t = keep.tile([P, T], U32, name="tab_w%d" % a)
-            nc.sync.dma_start(t[:].bitcast(I32), tab_words[a].rearrange("p t i -> p (t i)").bitcast(I32))
+            src = tab_words[a].rearrange("p t i -> p (t i)").bitcast(I32)
+            step = T // parts
+            for c in range(0, T, step):
+                nc.sync.dma_start(t[:, c : c + step].bitcast(I32), src[:, c : c + step])
             return t
 
         def load_wa_pass(dst, a, c0, width):
@@ -85,6 +85,12 @@ def tile_list_trap_spray_scores_kernel(
             )
             return t
 
+        def load_vector(src, name):
+            t = keep.tile([P, P], F32, name=name)
+            nc.vector.memset(t[:], 0.0)
+            nc.sync.dma_start(t[0:SLICES, :], src.rearrange("(s q) -> s q", q=P))
+            return t
+
         def load_rows(src, i, name):
             t = keep.tile([P, src.shape[1]], F32, name=name)
             nc.sync.dma_start(t[:], src[P * i : P * (i + 1), :])
@@ -94,10 +100,16 @@ def tile_list_trap_spray_scores_kernel(
         wa_raw = {}
         pages = []
 
-        def take_wd(s0, count):
-            t = load_wd("wd_w%d" % s0, P * s0, P * count)
+        def take_wd_words(s0, count):
+            wd_w[s0] = load_wd("wd_w%d" % s0, P * s0, P * count)
+
+        def take_wd_scales(s0, count):
+            t = wd_w[s0]
+            plane = keep.tile([P, KP * P * count], U8, name="wd_s%d" % s0, align_bytes=64)
+            nc.vector.memset(plane[:].bitcast(I32), 0)
+            load_scales(plane, wd_scales[:, :, P * s0 : P * (s0 + count)])
             for i in range(count):
-                wd_w[s0 + i] = (t, P * i)
+                wd_w[s0 + i] = (t, plane[:].rearrange("p (a c) -> p a c", a=KP), P * i)
 
         def take_wa(s0, count):
             t = load_wa(keep, "wa_raw%d" % s0, P * s0, P * count)
@@ -107,29 +119,30 @@ def tile_list_trap_spray_scores_kernel(
         def take_page(s):
             pages.append(load_rows(page0, s, "page0_%d" % s))
 
+        tab_w = [load_table(0, 4)]
         list1 = load_list(offs, "list1")
         list2 = load_list(offs2, "list2")
         list3 = load_list(offs3, "list3")
-        list4 = load_list(offs4, "list4")
-        tab_w = [load_table(0)]
-        nc.sync.dma_start(rows[0:SLICES, :], gain.rearrange("(s q) -> s q", q=P))
-        nc.sync.dma_start(rows[SLICES : 2 * SLICES, :], base.rearrange("(s q) -> s q", q=P))
-        take_wd(0, 4)
-        load_scales(nc.sync, tab_s, tab_scales)
         tab_w.append(load_table(1))
-        load_scales(nc.sync, wd_s, wd_scales)
+        load_scales(tab_s, tab_scales)
         tab_w.append(load_table(2))
+        take_wd_words(0, 2)
+        gain_rows = load_vector(gain, "gain_rows")
         wa_first = []
         for a in range(KP):
             t = keep.tile([P, 4, 2 * P], F32, name="wa_first%d" % a)
             load_wa_pass(t[:], a, 0, 2 * P)
             wa_first.append(t)
+            if a == 0:
+                take_wd_scales(0, 2)
+        base_rows = load_vector(base, "base_rows")
         wgs_t = load_rows(wgs, 0, "wgs_t")
         take_page(0)
         take_wa(2, 2)
+        take_wd_words(2, 6)
+        take_wd_scales(2, 6)
         take_page(1)
         take_page(2)
-        take_wd(4, 4)
         take_wa(4, 2)
         take_page(3)
         take_page(4)
@@ -139,7 +152,8 @@ def tile_list_trap_spray_scores_kernel(
         take_page(7)
         wy_w = keep.tile([P, RP, N], U32, name="wy_w", align_bytes=64)
         nc.sync.dma_start(wy_w[:].bitcast(I32), wy_words.rearrange("a p c i -> p a (c i)").bitcast(I32))
-        load_scales(nc.sync, wy_s, wy_scales)
+        load_scales(wy_s, wy_scales)
+        list4 = load_list(offs4, "list4")
         wgo_t = load_rows(wgo, 0, "wgo_t")
         res = []
         outs = []
@@ -148,10 +162,14 @@ def tile_list_trap_spray_scores_kernel(
         for i in range(NT):
             outs.append(load_rows(page1, i, "page1_%d" % i))
 
-        cols_ps = psum.tile([P, P], F32, name="cols_ps", tag="U0")
-        nc.tensor.transpose(cols_ps[:], rows[:], ident32[:])
-        cols = keep.tile([P, 2 * SLICES], F32, name="cols")
-        nc.scalar.copy(cols[:], cols_ps[:, 0 : 2 * SLICES])
+        def onto_partitions(rows, name, tag):
+            ps = psum.tile([P, P], F32, name="cols_ps", tag=tag)
+            nc.tensor.transpose(ps[:], rows[:], ident32[:])
+            cols = keep.tile([P, SLICES], F32, name=name)
+            nc.scalar.copy(cols[:], ps[:, 0:SLICES])
+            return cols
+
+        gain_cols = onto_partitions(gain_rows, "gain_cols", "U0")
 
         v_s = []
         v_w = []
@@ -164,42 +182,36 @@ def tile_list_trap_spray_scores_kernel(
             nc.vector.tensor_copy(t[:], tab_w[a][:].indirect(list1[:]))
             v_w.append(t)
 
-        def pinned(kind, s, at, shape, dtype):
-            return pin.tile(shape, dtype, name="%s%d" % (kind, s % 2), offset=3072 * (s % 2) + at, align_bytes=64)
-
         def held(kind, at, shape, dtype):
-            return pin.tile(shape, dtype, name=kind, offset=6144 + at, align_bytes=64)
+            return pin.tile(shape, dtype, name=kind, offset=at, align_bytes=64)
 
-        wa_b = {}
+        stage = {}
         wa_q = {}
 
         def round_wa(s):
-            lead = pinned("wb_lead", s, 512, [P, 2, P, 4], BF16)
-            rest = ring2.tile([P, P, 4], BF16, name="wb_rest", align_bytes=64)
+            wb = ring2.tile([P, KP * 4 * P], BF16, name="stage", align_bytes=64)
+            stage[s] = wb
             if s < 2:
                 for a in range(KP):
-                    dst = (lead[:, a] if a < 2 else rest[:]).rearrange("p (c i) j -> p c j i", i=4)
-                    src = wa_first[a][:, :, P * s : P * (s + 1)].rearrange("p j (c i) -> p c j i", i=4)
-                    nc.vector.tensor_copy(dst, src)
-            else:
+                    nc.vector.tensor_copy(
+                        wb[:, 512 * a : 512 * (a + 1)].rearrange("p (c i j) -> p c j i", i=4, j=4),
+                        wa_first[a][:, :, P * s : P * (s + 1)].rearrange("p j (c i) -> p c j i", i=4),
+                    )
+            elif s < SLICES:
                 raw, c0 = wa_raw[s]
-                src = raw[:, :, :, c0 : c0 + P].rearrange("p a j (c i) -> p a c j i", i=4)
-                nc.scalar.copy(rest[:].rearrange("p (c i) j -> p c j i", i=4), src[:, 2])
-                nc.scalar.copy(lead[:].rearrange("p a (c i) j -> p a c j i", i=4), src[:, 0:2])
-            wa_b[s] = (lead, rest)
+                nc.scalar.copy(
+                    wb[:].rearrange("p (a c i j) -> p a c j i", a=KP, i=4, j=4),
+                    raw[:, :, :, c0 : c0 + P].rearrange("p a j (c i) -> p a c j i", i=4),
+                )
 
         def quantise_wa(s):
             codes = ring2.tile([P, KP * P], U32, name="wa_codes", align_bytes=64)
             scales = ring2.tile([P, KP * P], U8, name="wa_scales", align_bytes=64)
-            lead, rest = wa_b[s]
-            parts = [
-                (0, 2 * P, lead[:].rearrange("p a c j -> p (a c j)")),
-                (2 * P, 3 * P, rest[:].rearrange("p c j -> p (c j)")),
-            ]
-            if s == 0:
-                parts[0:1] = [(P * a, P * (a + 1), lead[:, a].rearrange("p c j -> p (c j)")) for a in range(2)]
-            for lo, hi, src in parts if s < 2 else reversed(parts):
-                nc.vector.quantize_mx(out=codes[:, lo:hi].bitcast(FP8X4), scales=scales[:, lo:hi], in_=src)
+            cuts = [0, P, 2 * P, 3 * P] if s == 0 else [0, 2 * P, 3 * P]
+            for lo, hi in zip(cuts, cuts[1:]):
+                nc.vector.quantize_mx(
+                    out=codes[:, lo:hi].bitcast(FP8X4), scales=scales[:, lo:hi], in_=stage[s][:, 4 * lo : 4 * hi]
+                )
             wa_q[s] = (codes, scales)
 
         damps = {}
@@ -207,13 +219,13 @@ def tile_list_trap_spray_scores_kernel(
         states = {}
 
         def make_damping(s):
-            wd_t, c0 = wd_w[s]
-            b_ps = psum.tile([P, S], F32, name="b_ps", tag=("A%d" if s in (2, 3) else "B%d") % (s % 2))
+            wd_t, wd_s, c0 = wd_w[s]
+            b_ps = psum.tile([P, S], F32, name="b_ps", tag={1: "U1", 2: "A0", 3: "A1"}.get(s, "B%d" % (s % 2)))
             for a in range(KP):
                 nc.tensor.matmul_mx(
                     out=b_ps[:],
                     lhsT=wd_t[:, a, 2 * c0 : 2 * (c0 + P)].bitcast(FP4X4),
-                    lhsT_scale=wd_s[:, a * H + P * s : a * H + P * (s + 1)],
+                    lhsT_scale=wd_s[:, a, c0 : c0 + P],
                     rhs=v_w[a][:].bitcast(FP8X4),
                     rhs_scale=v_s[a][:],
                     start=(a == 0),
@@ -229,7 +241,10 @@ def tile_list_trap_spray_scores_kernel(
 
         def make_response(s):
             codes, scales = wa_q[s]
-            resp = ring2.tile([P, S], F32, name="resp")
+            if s == 0:
+                resp = stage[0][:, 0 : 2 * S].bitcast(F32)
+            else:
+                resp = ring2.tile([P, S], F32, name="resp")
             for lo, hi in spans(s):
                 a_ps = psum.tile([P, hi - lo], F32, name="a_ps", tag="U1" if lo else "A%d" % (s % 2))
                 for a in range(KP):
@@ -249,10 +264,10 @@ def tile_list_trap_spray_scores_kernel(
             if s == SLICES - 1:
                 h = held("h_last", 0, [P, S], F32)
             else:
-                h = pinned("h", s + 1, 0, [P, S], F32)
+                h = stage[s + 1][:, 0 : 2 * S].bitcast(F32)
             for lo, hi in spans(s):
                 nc.vector.scalar_tensor_tensor(
-                    h[:, lo:hi], resps[s][:, lo:hi], cols[:, s : s + 1], damps[s][:, lo:hi], ALU.mult, ALU.mult
+                    h[:, lo:hi], resps[s][:, lo:hi], gain_cols[:, s : s + 1], damps[s][:, lo:hi], ALU.mult, ALU.mult
                 )
             states[s] = h
 
@@ -266,7 +281,7 @@ def tile_list_trap_spray_scores_kernel(
             nc.vector.tensor_copy(picked, pages[s][:].indirect(list3[:, lo // 16 : hi // 16]))
 
         def bound(s, x, picked):
-            nc.vector.tensor_scalar(x, picked, cols[:, SLICES + s : SLICES + s + 1], None, ALU.max)
+            nc.vector.tensor_scalar(x, picked, base_cols[:, s : s + 1], None, ALU.max)
 
         def turn(s, x, x_t, blocks, tag):
             ps = psum.tile([P, blocks, P], BF16, name="turn_ps", tag=tag)
@@ -290,6 +305,7 @@ def tile_list_trap_spray_scores_kernel(
         x_t0 = keep.tile([P, 4, 512], BF16, name="x_t0")
         x_t1 = [keep.tile([P, 2, 512], BF16, name="x_t1%d" % i) for i in range(2)]
         x0_w = keep.tile([P, M], U32, name="x0_w", align_bytes=64)
+        x0_s = keep.tile([P, M], U8, name="x0_s", align_bytes=64)
         x1_w = [keep.tile([P, HALF], U32, name="x1_w%d" % i, align_bytes=64) for i in range(2)]
         x1_s = [keep.tile([P, HALF], U8, name="x1_s%d" % i, align_bytes=64) for i in range(2)]
 
@@ -297,6 +313,7 @@ def tile_list_trap_spray_scores_kernel(
         round_wa(0)
         quantise_wa(0)
         make_response(0)
+        base_cols = onto_partitions(base_rows, "base_cols", "A0")
         round_wa(1)
         quantise_wa(1)
         make_states(0)
@@ -305,23 +322,23 @@ def tile_list_trap_spray_scores_kernel(
         round_wa(2)
         for s in range(SLICES - 1):
             put_states(s)
+            if s + 2 < SLICES:
+                quantise_wa(s + 2)
             width = M if s < 4 else HALF
             picked = ring2.tile([P, M], F32, name="picked")
             recall(s, picked[:, 0:width], 0, width)
-            if s + 2 < SLICES:
-                quantise_wa(s + 2)
             make_states(s + 1)
-            x = pinned("x", s, 2048, [P, M], BF16)
+            x = stage[s + 2][:, 2 * S : 3 * S]
             bound(s, x[:, 0:width], picked[:, 0:width])
             if s + 2 < SLICES:
                 make_damping(s + 2)
                 make_response(s + 2)
-            if s + 3 < SLICES:
                 round_wa(s + 3)
             turn(s, x, x_t0 if s < 4 else x_t1[0], width // P, "Y%d" % (s % 2))
             if s == 3:
                 for i in range(2):
                     turn_back(x_t0, 2 * i, grouped0[:, 4 * HALF * i : 4 * HALF * (i + 1)], "U%d" % i)
+                nc.vector.quantize_mx(out=x0_w[:].bitcast(FP8X4), scales=x0_s[:], in_=grouped0[:])
         put_states(SLICES - 1)
 
         pieces = [([0], 2 * P, 4 * P), ([1], 2 * P, 4 * P), ([2, 3], 0, 2 * P), ([2], 2 * P, 4 * P), ([3], 2 * P, 4 * P)]
@@ -333,7 +350,7 @@ def tile_list_trap_spray_scores_kernel(
 
         res_t = keep.tile([P, len(pieces), 4 * P], F32, name="res_t", tag="wa_raw2")
         for k, (blocks, n0, count) in enumerate(pieces):
-            ps = psum.tile([P, 4 * P], F32, name="rt_ps", tag="U%d" % (k % 2))
+            ps = psum.tile([P, 4 * P], F32, name="rt_ps", tag="B%d" % (k % 2))
             for mb in blocks:
                 for i in range(n0 // P, (n0 + count) // P):
                     at = place(mb, i)[1]
@@ -353,12 +370,10 @@ def tile_list_trap_spray_scores_kernel(
 
         late = held("late", 1024, [P, 4, HALF], F32)
         recall_half(7, late[:, 0, :], 0, "B0")
-        x0_s = held("x0_s", 0, [P, M], U8)
-        nc.vector.quantize_mx(out=x0_w[:].bitcast(FP8X4), scales=x0_s[:], in_=grouped0[:])
         quantise_half(0, "hold2")
         for s in range(4, 7):
             recall_half(s, late[:, s - 3, :], 1, "U0")
-        last = keep.tile([P, HALF], F32, name="last", tag="hold2", align_bytes=64)
+        last = keep.tile([P, HALF], F32, name="last")
         recall_half(7, last[:], 1, "B0")
 
         y_t = keep.tile([P, len(pieces), 4 * P], F32, name="y_t", tag="wa_raw4")

@@ -216,11 +216,11 @@ def tile_list_trap_spray_scores_kernel(
 
         damps = {}
         resps = {}
-        states = {}
+        weights = {}
 
         def make_damping(s):
             wd_t, wd_s, c0 = wd_w[s]
-            b_ps = psum.tile([P, S], F32, name="b_ps", tag={1: "U1", 2: "A0", 3: "A1"}.get(s, "B%d" % (s % 2)))
+            b_ps = psum.tile([P, S], F32, name="b_ps", tag={2: "B0", 3: "A1"}.get(s, "B%d" % (s % 2)))
             for a in range(KP):
                 nc.tensor.matmul_mx(
                     out=b_ps[:],
@@ -231,51 +231,52 @@ def tile_list_trap_spray_scores_kernel(
                     start=(a == 0),
                     stop=(a == KP - 1),
                 )
-            damp = ring2.tile([P, S], F32, name="damp")
+            if s == 1:
+                damp = stage[1][:, 0 : 2 * S].bitcast(F32)
+            else:
+                damp = ring2.tile([P, S], F32, name="damp")
             nc.scalar.activation(damp[:], b_ps[:], ACT.Abs)
             nc.scalar.activation(damp[:], damp[:], ACT.Exp, scale=-1.0)
             damps[s] = damp
 
-        def spans(s):
-            return [(0, S // 2), (S // 2, S)] if s == 0 else [(0, S)]
-
         def make_response(s):
             codes, scales = wa_q[s]
+            a_ps = psum.tile([P, S], F32, name="a_ps", tag="B0" if s == 0 else "A%d" % (s % 2))
+            for a in range(KP):
+                nc.tensor.matmul_mx(
+                    out=a_ps[:],
+                    lhsT=codes[:, P * a : P * (a + 1)].bitcast(FP8X4),
+                    lhsT_scale=scales[:, P * a : P * (a + 1)],
+                    rhs=v_w[a][:].bitcast(FP8X4),
+                    rhs_scale=v_s[a][:],
+                    start=(a == 0),
+                    stop=(a == KP - 1),
+                )
             if s == 0:
                 resp = stage[0][:, 0 : 2 * S].bitcast(F32)
             else:
                 resp = ring2.tile([P, S], F32, name="resp")
-            for lo, hi in spans(s):
-                a_ps = psum.tile([P, hi - lo], F32, name="a_ps", tag="U1" if lo else "A%d" % (s % 2))
-                for a in range(KP):
-                    nc.tensor.matmul_mx(
-                        out=a_ps[:],
-                        lhsT=codes[:, P * a : P * (a + 1)].bitcast(FP8X4),
-                        lhsT_scale=scales[:, P * a : P * (a + 1)],
-                        rhs=v_w[a][:, lo:hi].bitcast(FP8X4),
-                        rhs_scale=v_s[a][:, lo:hi],
-                        start=(a == 0),
-                        stop=(a == KP - 1),
-                    )
-                nc.scalar.activation(resp[:, lo:hi], a_ps[:], ACT.Tanh)
+            nc.scalar.activation(resp[:], a_ps[:], ACT.Tanh)
             resps[s] = resp
 
-        def make_states(s):
-            if s == SLICES - 1:
-                h = held("h_last", 0, [P, S], F32)
+        def make_weight(s):
+            if s == 1:
+                weight = weights[0]
+            elif s == SLICES - 1:
+                weight = held("weight_last", 0, [P, S], F32)
             else:
-                h = stage[s + 1][:, 0 : 2 * S].bitcast(F32)
-            for lo, hi in spans(s):
-                nc.vector.scalar_tensor_tensor(
-                    h[:, lo:hi], resps[s][:, lo:hi], gain_cols[:, s : s + 1], damps[s][:, lo:hi], ALU.mult, ALU.mult
-                )
-            states[s] = h
+                weight = ring2.tile([P, S], F32, name="weight")
+            gain_s = gain_cols[:, s : s + 1]
+            if s < 2:
+                nc.vector.scalar_tensor_tensor(weight[:], damps[s][:], gain_s, wgs_t[:], ALU.mult, ALU.mult)
+            else:
+                factor = ring2.tile([P, S], F32, name="factor")
+                nc.scalar.activation(factor[:], wgs_t[:], ACT.Copy, scale=gain_s)
+                nc.gpsimd.tensor_tensor(weight[:], damps[s][:], factor[:], ALU.mult)
+            weights[s] = weight
 
         def put_states(s):
-            for lo, hi in spans(s):
-                nc.vector.tensor_tensor(
-                    pages[s][:].indirect(list2[:, lo // 16 : hi // 16]), states[s][:, lo:hi], wgs_t[:, lo:hi], ALU.mult
-                )
+            nc.vector.tensor_tensor(pages[s][:].indirect(list2[:]), resps[s][:], weights[s][:], ALU.mult)
 
         def recall(s, picked, lo, hi):
             nc.vector.tensor_copy(picked, pages[s][:].indirect(list3[:, lo // 16 : hi // 16]))
@@ -312,28 +313,33 @@ def tile_list_trap_spray_scores_kernel(
         make_damping(0)
         round_wa(0)
         quantise_wa(0)
-        make_response(0)
-        base_cols = onto_partitions(base_rows, "base_cols", "A0")
         round_wa(1)
         quantise_wa(1)
-        make_states(0)
+        make_weight(0)
         make_damping(1)
+        make_response(0)
+        base_cols = onto_partitions(base_rows, "base_cols", "B0")
         make_response(1)
         round_wa(2)
+        make_damping(2)
+        make_weight(2)
         for s in range(SLICES - 1):
             put_states(s)
+            if s == 0:
+                make_weight(1)
             if s + 2 < SLICES:
                 quantise_wa(s + 2)
             width = M if s < 4 else HALF
             picked = ring2.tile([P, M], F32, name="picked")
             recall(s, picked[:, 0:width], 0, width)
-            make_states(s + 1)
             x = stage[s + 2][:, 2 * S : 3 * S]
             bound(s, x[:, 0:width], picked[:, 0:width])
+            if s + 3 < SLICES:
+                make_damping(s + 3)
+                make_weight(s + 3)
             if s + 2 < SLICES:
-                make_damping(s + 2)
-                make_response(s + 2)
                 round_wa(s + 3)
+                make_response(s + 2)
             turn(s, x, x_t0 if s < 4 else x_t1[0], width // P, "Y%d" % (s % 2))
             if s == 3:
                 for i in range(2):
@@ -368,7 +374,7 @@ def tile_list_trap_spray_scores_kernel(
             turn_back(x_t1[i], 0, grouped[:], "U%d" % i)
             nc.vector.quantize_mx(out=x1_w[i][:].bitcast(FP8X4), scales=x1_s[i][:], in_=grouped[:])
 
-        late = held("late", 1024, [P, 4, HALF], F32)
+        late = held("late", 0, [P, 4, HALF], F32)
         recall_half(7, late[:, 0, :], 0, "B0")
         quantise_half(0, "hold2")
         for s in range(4, 7):

@@ -14,15 +14,28 @@ FP4X4 = mybir.dt.float4_e2m1fn_x4
 ACT = mybir.ActivationFunctionType
 ALU = mybir.AluOpType
 
-K, T, S, H, T2, N, M = 1536, 2048, 512, 1024, 1024, 768, 512
+K, T, S, H, N, M = 1536, 2048, 512, 1024, 768, 512
 P = 128
-KP = K // 512
-RP = H // 512
+PACK = 4
+PASS = P * PACK
+K_PASSES = K // PASS
+R_PASSES = H // PASS
 SLICES = H // P
-NT = N // P
+PASS_SLICES = PASS // P
+N_TILES = N // P
 HALF = M // 2
-PASS_ORDER = (0, 1)
+HEAD = 2
+DIRECT = 2
 FLOPS = 2 * K * H * S * 2 + 2 * H * N * M
+
+UPPER = (DIRECT * P, N - DIRECT * P)
+PIECES = [([0],) + UPPER, ([1],) + UPPER, ([2, 3], 0, DIRECT * P), ([2],) + UPPER, ([3],) + UPPER]
+
+
+def place(mb, i):
+    for k, (blocks, n0, count) in enumerate(PIECES):
+        if mb in blocks and n0 <= P * i < n0 + count:
+            return k, count * blocks.index(mb) + P * i - n0
 
 
 def tile_list_trap_spray_scores_kernel(
@@ -34,7 +47,6 @@ def tile_list_trap_spray_scores_kernel(
         keep = ctx.enter_context(tc.tile_pool(name="keep", bufs=1))
         ring2 = ctx.enter_context(tc.tile_pool(name="ring2", bufs=2))
         ring3 = ctx.enter_context(tc.tile_pool(name="ring3", bufs=3))
-        pin = ctx.enter_context(tc.tile_pool(name="pin", bufs=1))
         psum = ctx.enter_context(tc.psum_pool(name="psum", bufs=1))
 
         def load_list(src, name):
@@ -42,26 +54,15 @@ def tile_list_trap_spray_scores_kernel(
             nc.sync.dma_start(t[:], src)
             return t
 
-        def load_scales(plane, src):
+        def load_scales(scales, src):
             passes = src.shape[0]
             for q in range(4):
                 nc.sync.dma_start(
-                    plane[32 * q : 32 * q + 4, :].bitcast(I32).rearrange("r (a c) -> r a c", a=passes),
+                    scales[32 * q : 32 * q + 4, :].bitcast(I32).rearrange("r (a c) -> r a c", a=passes),
                     src[:, 4 * q : 4 * q + 4, :].bitcast(I32).rearrange("a r c -> r a c"),
                 )
 
-        tab_s = keep.tile([P, KP * T], U8, name="tab_s", align_bytes=64)
-        wy_s = keep.tile([P, RP * N], U8, name="wy_s", align_bytes=64)
-        nc.gpsimd.memset(tab_s[:, 0 : KP * T // 2].bitcast(I32), 0)
-        nc.vector.memset(tab_s[:, KP * T // 2 : KP * T].bitcast(I32), 0)
-        nc.vector.memset(wy_s[:].bitcast(I32), 0)
-
-        ident32 = keep.tile([P, P], F32, name="ident32")
-        make_identity(nc, ident32[:])
-        ident16 = keep.tile([P, P], BF16, name="ident16")
-        nc.scalar.copy(ident16[:], ident32[:])
-
-        def load_table(a, parts=1):
+        def load_table(a, parts):
             t = keep.tile([P, T], U32, name="tab_w%d" % a)
             src = tab_words[a].rearrange("p t i -> p (t i)").bitcast(I32)
             step = T // parts
@@ -69,21 +70,27 @@ def tile_list_trap_spray_scores_kernel(
                 nc.sync.dma_start(t[:, c : c + step].bitcast(I32), src[:, c : c + step])
             return t
 
-        def load_wa_pass(dst, a, c0, width):
-            nc.sync.dma_start(dst, wa[512 * a : 512 * (a + 1), c0 : c0 + width].rearrange("(p j) c -> p j c", j=4))
+        def load_wa_pass(dst, a, s0):
+            rows = wa[PASS * a : PASS * (a + 1), P * s0 : P * (s0 + 2)]
+            nc.sync.dma_start(dst, rows.rearrange("(p j) c -> p j c", j=PACK))
 
-        def load_wa(pool, tag, c0, width):
-            t = pool.tile([P, KP, 4, width], F32, name=tag)
-            for a in range(KP):
-                load_wa_pass(t[:, a], a, c0, width)
+        def load_wa_pair(s0):
+            t = keep.tile([P, K_PASSES, PACK, 2 * P], F32, name="wa_raw%d" % s0)
+            for a in range(K_PASSES):
+                load_wa_pass(t[:, a], a, s0)
             return t
 
-        def load_wd(name, c0, width):
-            t = keep.tile([P, KP, 2 * width], U8, name=name, align_bytes=64)
-            nc.sync.dma_start(
-                t[:].bitcast(I32), wd_words[:, :, 2 * c0 : 2 * (c0 + width)].bitcast(I32).rearrange("a p c -> p a c")
-            )
+        def load_wd_words(s0, count):
+            t = keep.tile([P, K_PASSES, 2 * P * count], U8, name="wd_w%d" % s0, align_bytes=64)
+            src = wd_words[:, :, 2 * P * s0 : 2 * P * (s0 + count)].bitcast(I32)
+            nc.sync.dma_start(t[:].bitcast(I32), src.rearrange("a p c -> p a c"))
             return t
+
+        def load_wd_scales(s0, count):
+            t = keep.tile([P, K_PASSES * P * count], U8, name="wd_s%d" % s0, align_bytes=64)
+            nc.vector.memset(t[:].bitcast(I32), 0)
+            load_scales(t, wd_scales[:, :, P * s0 : P * (s0 + count)])
+            return t[:].rearrange("p (a c) -> p a c", a=K_PASSES)
 
         def load_vector(src, name):
             t = keep.tile([P, P], F32, name=name)
@@ -96,74 +103,53 @@ def tile_list_trap_spray_scores_kernel(
             nc.sync.dma_start(t[:], src[P * i : P * (i + 1), :])
             return t
 
-        wd_w = {}
-        wa_raw = {}
-        pages = []
+        tab_s = keep.tile([P, K_PASSES * T], U8, name="tab_s", align_bytes=64)
+        wy_s = keep.tile([P, R_PASSES * N], U8, name="wy_s", align_bytes=64)
+        nc.gpsimd.memset(tab_s[:, 0 : K_PASSES * T // 2].bitcast(I32), 0)
+        nc.vector.memset(tab_s[:, K_PASSES * T // 2 : K_PASSES * T].bitcast(I32), 0)
+        nc.vector.memset(wy_s[:].bitcast(I32), 0)
 
-        def take_wd_words(s0, count):
-            wd_w[s0] = load_wd("wd_w%d" % s0, P * s0, P * count)
-
-        def take_wd_scales(s0, count):
-            t = wd_w[s0]
-            plane = keep.tile([P, KP * P * count], U8, name="wd_s%d" % s0, align_bytes=64)
-            nc.vector.memset(plane[:].bitcast(I32), 0)
-            load_scales(plane, wd_scales[:, :, P * s0 : P * (s0 + count)])
-            for i in range(count):
-                wd_w[s0 + i] = (t, plane[:].rearrange("p (a c) -> p a c", a=KP), P * i)
-
-        def take_wa(s0, count):
-            t = load_wa(keep, "wa_raw%d" % s0, P * s0, P * count)
-            for i in range(count):
-                wa_raw[s0 + i] = (t, P * i)
-
-        def take_page(s):
-            pages.append(load_rows(page0, s, "page0_%d" % s))
+        ident32 = keep.tile([P, P], F32, name="ident32")
+        make_identity(nc, ident32[:])
+        ident16 = keep.tile([P, P], BF16, name="ident16")
+        nc.scalar.copy(ident16[:], ident32[:])
 
         tab_w = [load_table(0, 4)]
         list1 = load_list(offs, "list1")
         list2 = load_list(offs2, "list2")
         list3 = load_list(offs3, "list3")
-        tab_w.append(load_table(1))
+        tab_w.append(load_table(1, 1))
         load_scales(tab_s, tab_scales)
-        tab_w.append(load_table(2))
-        take_wd_words(0, 2)
+        tab_w.append(load_table(2, 1))
+        wd_head_w = load_wd_words(0, HEAD)
         gain_rows = load_vector(gain, "gain_rows")
-        wa_first = []
-        for a in range(KP):
-            t = keep.tile([P, 4, 2 * P], F32, name="wa_first%d" % a)
-            load_wa_pass(t[:], a, 0, 2 * P)
-            wa_first.append(t)
-            if a == 0:
-                take_wd_scales(0, 2)
+        wa_head = [keep.tile([P, PACK, HEAD * P], F32, name="wa_head%d" % a) for a in range(K_PASSES)]
+        load_wa_pass(wa_head[0][:], 0, 0)
+        wd_head_s = load_wd_scales(0, HEAD)
+        for a in range(1, K_PASSES):
+            load_wa_pass(wa_head[a][:], a, 0)
         base_rows = load_vector(base, "base_rows")
         wgs_t = load_rows(wgs, 0, "wgs_t")
-        take_page(0)
-        take_wa(2, 2)
-        take_wd_words(2, 6)
-        take_wd_scales(2, 6)
-        take_page(1)
-        take_page(2)
-        take_wa(4, 2)
-        take_page(3)
-        take_page(4)
-        take_wa(6, 2)
-        take_page(5)
-        take_page(6)
-        take_page(7)
-        wy_w = keep.tile([P, RP, N], U32, name="wy_w", align_bytes=64)
+        pages = [load_rows(page0, 0, "page0_0")]
+        wa_raw = {}
+        for s0 in range(HEAD, SLICES, 2):
+            wa_raw[s0] = load_wa_pair(s0)
+            if s0 == HEAD:
+                wd_rest_w = load_wd_words(HEAD, SLICES - HEAD)
+                wd_rest_s = load_wd_scales(HEAD, SLICES - HEAD)
+            for s in (s0 - 1, s0):
+                pages.append(load_rows(page0, s, "page0_%d" % s))
+        pages.append(load_rows(page0, SLICES - 1, "page0_last"))
+        wy_w = keep.tile([P, R_PASSES, N], U32, name="wy_w", align_bytes=64)
         nc.sync.dma_start(wy_w[:].bitcast(I32), wy_words.rearrange("a p c i -> p a (c i)").bitcast(I32))
         load_scales(wy_s, wy_scales)
         list4 = load_list(offs4, "list4")
         wgo_t = load_rows(wgo, 0, "wgo_t")
-        res = []
-        outs = []
-        for i in range(NT):
-            res.append(load_rows(resid, i, "res%d" % i))
-        for i in range(NT):
-            outs.append(load_rows(page1, i, "page1_%d" % i))
+        res = [load_rows(resid, i, "res%d" % i) for i in range(N_TILES)]
+        outs = [load_rows(page1, i, "page1_%d" % i) for i in range(N_TILES)]
 
-        def onto_partitions(rows, name, tag):
-            ps = psum.tile([P, P], F32, name="cols_ps", tag=tag)
+        def onto_partitions(rows, name, bank):
+            ps = psum.tile([P, P], F32, name="cols_ps", tag=bank)
             nc.tensor.transpose(ps[:], rows[:], ident32[:])
             cols = keep.tile([P, SLICES], F32, name=name)
             nc.scalar.copy(cols[:], ps[:, 0:SLICES])
@@ -171,108 +157,89 @@ def tile_list_trap_spray_scores_kernel(
 
         gain_cols = onto_partitions(gain_rows, "gain_cols", "U0")
 
-        v_s = []
-        v_w = []
-        for a in range(KP):
-            t = keep.tile([P, S], U8, name="v_s%d" % a, align_bytes=64)
-            nc.vector.tensor_copy(t[:], tab_s[:, a * T : (a + 1) * T].indirect(list1[:]))
-            v_s.append(t)
-        for a in range(KP):
-            t = keep.tile([P, S], U32, name="v_w%d" % a, align_bytes=64)
-            nc.vector.tensor_copy(t[:], tab_w[a][:].indirect(list1[:]))
-            v_w.append(t)
+        v_s = [keep.tile([P, S], U8, name="v_s%d" % a, align_bytes=64) for a in range(K_PASSES)]
+        v_w = [keep.tile([P, S], U32, name="v_w%d" % a, align_bytes=64) for a in range(K_PASSES)]
+        for a in range(K_PASSES):
+            nc.vector.tensor_copy(v_s[a][:], tab_s[:, a * T : (a + 1) * T].indirect(list1[:]))
+        for a in range(K_PASSES):
+            nc.vector.tensor_copy(v_w[a][:], tab_w[a][:].indirect(list1[:]))
 
-        def held(kind, at, shape, dtype):
-            return pin.tile(shape, dtype, name=kind, offset=at, align_bytes=64)
+        stage, wa_q, damps, resps, weights = {}, {}, {}, {}, {}
 
-        stage = {}
-        wa_q = {}
+        def open_stage(s):
+            stage[s] = ring2.tile([P, K_PASSES * PASS], BF16, name="stage", align_bytes=64)
+
+        def front_of_stage(s):
+            return stage[s][:, 0 : 2 * S].bitcast(F32)
 
         def round_wa(s):
-            wb = ring2.tile([P, KP * 4 * P], BF16, name="stage", align_bytes=64)
-            stage[s] = wb
-            if s < 2:
-                for a in range(KP):
+            open_stage(s)
+            if s < HEAD:
+                for a in range(K_PASSES):
                     nc.vector.tensor_copy(
-                        wb[:, 512 * a : 512 * (a + 1)].rearrange("p (c i j) -> p c j i", i=4, j=4),
-                        wa_first[a][:, :, P * s : P * (s + 1)].rearrange("p j (c i) -> p c j i", i=4),
+                        stage[s][:, PASS * a : PASS * (a + 1)].rearrange("p (c i j) -> p c j i", i=4, j=PACK),
+                        wa_head[a][:, :, P * s : P * (s + 1)].rearrange("p j (c i) -> p c j i", i=4),
                     )
-            elif s < SLICES:
-                raw, c0 = wa_raw[s]
+            else:
+                c0 = P * (s % 2)
                 nc.scalar.copy(
-                    wb[:].rearrange("p (a c i j) -> p a c j i", a=KP, i=4, j=4),
-                    raw[:, :, :, c0 : c0 + P].rearrange("p a j (c i) -> p a c j i", i=4),
+                    stage[s][:].rearrange("p (a c i j) -> p a c j i", a=K_PASSES, i=4, j=PACK),
+                    wa_raw[s - s % 2][:, :, :, c0 : c0 + P].rearrange("p a j (c i) -> p a c j i", i=4),
                 )
 
         def quantise_wa(s):
-            codes = ring2.tile([P, KP * P], U32, name="wa_codes", align_bytes=64)
-            scales = ring2.tile([P, KP * P], U8, name="wa_scales", align_bytes=64)
+            codes = ring2.tile([P, K_PASSES * P], U32, name="wa_codes", align_bytes=64)
+            scales = ring2.tile([P, K_PASSES * P], U8, name="wa_scales", align_bytes=64)
             cuts = [0, P, 2 * P, 3 * P] if s == 0 else [0, 2 * P, 3 * P]
             for lo, hi in zip(cuts, cuts[1:]):
                 nc.vector.quantize_mx(
-                    out=codes[:, lo:hi].bitcast(FP8X4), scales=scales[:, lo:hi], in_=stage[s][:, 4 * lo : 4 * hi]
+                    out=codes[:, lo:hi].bitcast(FP8X4), scales=scales[:, lo:hi], in_=stage[s][:, PACK * lo : PACK * hi]
                 )
             wa_q[s] = (codes, scales)
 
-        damps = {}
-        resps = {}
-        weights = {}
-
         def make_damping(s):
-            wd_t, wd_s, c0 = wd_w[s]
-            b_ps = psum.tile([P, S], F32, name="b_ps", tag={2: "B0", 3: "A1"}.get(s, "B%d" % (s % 2)))
-            for a in range(KP):
+            words, scales, c0 = (wd_head_w, wd_head_s, P * s) if s < HEAD else (wd_rest_w, wd_rest_s, P * (s - HEAD))
+            ps = psum.tile([P, S], F32, name="b_ps", tag="A1" if s == HEAD + 1 else "B%d" % (s % 2))
+            for a in range(K_PASSES):
                 nc.tensor.matmul_mx(
-                    out=b_ps[:],
-                    lhsT=wd_t[:, a, 2 * c0 : 2 * (c0 + P)].bitcast(FP4X4),
-                    lhsT_scale=wd_s[:, a, c0 : c0 + P],
+                    out=ps[:],
+                    lhsT=words[:, a, 2 * c0 : 2 * (c0 + P)].bitcast(FP4X4),
+                    lhsT_scale=scales[:, a, c0 : c0 + P],
                     rhs=v_w[a][:].bitcast(FP8X4),
                     rhs_scale=v_s[a][:],
                     start=(a == 0),
-                    stop=(a == KP - 1),
+                    stop=(a == K_PASSES - 1),
                 )
-            if s == 1:
-                damp = stage[1][:, 0 : 2 * S].bitcast(F32)
-            else:
-                damp = ring2.tile([P, S], F32, name="damp")
-            nc.scalar.activation(damp[:], b_ps[:], ACT.Abs)
+            damp = ring2.tile([P, S], F32, name="damp")
+            nc.scalar.activation(damp[:], ps[:], ACT.Abs)
             nc.scalar.activation(damp[:], damp[:], ACT.Exp, scale=-1.0)
             damps[s] = damp
 
         def make_response(s):
             codes, scales = wa_q[s]
-            a_ps = psum.tile([P, S], F32, name="a_ps", tag="B0" if s == 0 else "A%d" % (s % 2))
-            for a in range(KP):
+            ps = psum.tile([P, S], F32, name="a_ps", tag="B0" if s == 0 else "A%d" % (s % 2))
+            for a in range(K_PASSES):
                 nc.tensor.matmul_mx(
-                    out=a_ps[:],
+                    out=ps[:],
                     lhsT=codes[:, P * a : P * (a + 1)].bitcast(FP8X4),
                     lhsT_scale=scales[:, P * a : P * (a + 1)],
                     rhs=v_w[a][:].bitcast(FP8X4),
                     rhs_scale=v_s[a][:],
                     start=(a == 0),
-                    stop=(a == KP - 1),
+                    stop=(a == K_PASSES - 1),
                 )
-            if s == 0:
-                resp = stage[0][:, 0 : 2 * S].bitcast(F32)
-            else:
-                resp = ring2.tile([P, S], F32, name="resp")
-            nc.scalar.activation(resp[:], a_ps[:], ACT.Tanh)
+            resp = front_of_stage(0) if s == 0 else ring2.tile([P, S], F32, name="resp")
+            nc.scalar.activation(resp[:], ps[:], ACT.Tanh)
             resps[s] = resp
 
         def make_weight(s):
-            if s == 1:
-                weight = weights[0]
-            elif s == SLICES - 1:
-                weight = held("weight_last", 0, [P, S], F32)
+            if s + 1 < SLICES:
+                weight = front_of_stage(s + 1)
             else:
-                weight = ring2.tile([P, S], F32, name="weight")
-            gain_s = gain_cols[:, s : s + 1]
-            if s < 2:
-                nc.vector.scalar_tensor_tensor(weight[:], damps[s][:], gain_s, wgs_t[:], ALU.mult, ALU.mult)
-            else:
-                factor = ring2.tile([P, S], F32, name="factor")
-                nc.scalar.activation(factor[:], wgs_t[:], ACT.Copy, scale=gain_s)
-                nc.gpsimd.tensor_tensor(weight[:], damps[s][:], factor[:], ALU.mult)
+                weight = keep.tile([P, S], F32, name="weight_last", tag="behind_last_scatter")
+            nc.vector.scalar_tensor_tensor(
+                weight[:], damps[s][:], gain_cols[:, s : s + 1], wgs_t[:], ALU.mult, ALU.mult
+            )
             weights[s] = weight
 
         def put_states(s):
@@ -284,126 +251,118 @@ def tile_list_trap_spray_scores_kernel(
         def bound(s, x, picked):
             nc.vector.tensor_scalar(x, picked, base_cols[:, s : s + 1], None, ALU.max)
 
-        def turn(s, x, x_t, blocks, tag):
-            ps = psum.tile([P, blocks, P], BF16, name="turn_ps", tag=tag)
+        def turn(s, x, x_t, blocks, bank):
+            ps = psum.tile([P, blocks, P], BF16, name="turn_ps", tag=bank)
             for mb in range(blocks):
                 nc.tensor.transpose(ps[:, mb, :], x[:, P * mb : P * (mb + 1)], ident16[:])
-            sl = s % 4
-            nc.scalar.copy(x_t[:, :, P * sl : P * (sl + 1)], ps[:])
+            c0 = P * (s % PASS_SLICES)
+            nc.scalar.copy(x_t[:, :, c0 : c0 + P], ps[:])
 
-        def turn_back(x_t, mb0, grouped, tag):
+        def turn_back(x_t, mb0, grouped, bank):
             words = x_t[:].bitcast(F32)
-            ps = psum.tile([P, 2, 2, P], F32, name="back_ps", tag=tag)
+            ps = psum.tile([P, 2, 2, P], F32, name="back_ps", tag=bank)
             for mb in range(2):
                 for u in range(2):
-                    nc.tensor.transpose(ps[:, mb, u, :], words[:, mb0 + mb, u : 256 : 2], ident32[:])
+                    nc.tensor.transpose(ps[:, mb, u, :], words[:, mb0 + mb, u : 2 * P : 2], ident32[:])
             nc.scalar.copy(
                 grouped.bitcast(F32).rearrange("p (b m u) -> p b m u", b=2, u=2),
                 ps[:].rearrange("p b u m -> p b m u"),
             )
 
-        grouped0 = keep.tile([P, 4 * M], BF16, name="grouped0", align_bytes=64)
-        x_t0 = keep.tile([P, 4, 512], BF16, name="x_t0")
-        x_t1 = [keep.tile([P, 2, 512], BF16, name="x_t1%d" % i) for i in range(2)]
+        grouped0 = keep.tile([P, PACK * M], BF16, name="grouped0", align_bytes=64)
+        x_t0 = keep.tile([P, M // P, PASS], BF16, name="x_t0")
+        x_t1 = [keep.tile([P, HALF // P, PASS], BF16, name="x_t1%d" % hf) for hf in range(2)]
         x0_w = keep.tile([P, M], U32, name="x0_w", align_bytes=64)
         x0_s = keep.tile([P, M], U8, name="x0_s", align_bytes=64)
-        x1_w = [keep.tile([P, HALF], U32, name="x1_w%d" % i, align_bytes=64) for i in range(2)]
-        x1_s = [keep.tile([P, HALF], U8, name="x1_s%d" % i, align_bytes=64) for i in range(2)]
+        x1_w = [keep.tile([P, HALF], U32, name="x1_w%d" % hf, align_bytes=64) for hf in range(2)]
+        x1_s = [keep.tile([P, HALF], U8, name="x1_s%d" % hf, align_bytes=64) for hf in range(2)]
 
-        make_damping(0)
-        round_wa(0)
-        quantise_wa(0)
-        round_wa(1)
-        quantise_wa(1)
-        make_weight(0)
-        make_damping(1)
-        make_response(0)
-        base_cols = onto_partitions(base_rows, "base_cols", "B0")
-        make_response(1)
-        round_wa(2)
-        make_damping(2)
-        make_weight(2)
-        for s in range(SLICES - 1):
-            put_states(s)
-            if s == 0:
-                make_weight(1)
-            if s + 2 < SLICES:
-                quantise_wa(s + 2)
-            width = M if s < 4 else HALF
-            picked = ring2.tile([P, M], F32, name="picked")
-            recall(s, picked[:, 0:width], 0, width)
-            x = stage[s + 2][:, 2 * S : 3 * S]
-            bound(s, x[:, 0:width], picked[:, 0:width])
-            if s + 3 < SLICES:
-                make_damping(s + 3)
-                make_weight(s + 3)
-            if s + 2 < SLICES:
-                round_wa(s + 3)
-                make_response(s + 2)
-            turn(s, x, x_t0 if s < 4 else x_t1[0], width // P, "Y%d" % (s % 2))
-            if s == 3:
-                for i in range(2):
-                    turn_back(x_t0, 2 * i, grouped0[:, 4 * HALF * i : 4 * HALF * (i + 1)], "U%d" % i)
-                nc.vector.quantize_mx(out=x0_w[:].bitcast(FP8X4), scales=x0_s[:], in_=grouped0[:])
-        put_states(SLICES - 1)
+        res_t = keep.tile([P, len(PIECES), PASS], F32, name="res_t", tag="wa_raw%d" % HEAD)
 
-        pieces = [([0], 2 * P, 4 * P), ([1], 2 * P, 4 * P), ([2, 3], 0, 2 * P), ([2], 2 * P, 4 * P), ([3], 2 * P, 4 * P)]
-
-        def place(mb, i):
-            for k, (blocks, n0, count) in enumerate(pieces):
-                if mb in blocks and n0 <= P * i < n0 + count:
-                    return k, count * blocks.index(mb) + P * i - n0
-
-        res_t = keep.tile([P, len(pieces), 4 * P], F32, name="res_t", tag="wa_raw2")
-        for k, (blocks, n0, count) in enumerate(pieces):
-            ps = psum.tile([P, 4 * P], F32, name="rt_ps", tag="B%d" % (k % 2))
+        def turn_residual(k):
+            blocks, n0, count = PIECES[k]
+            ps = psum.tile([P, PASS], F32, name="rt_ps", tag="B%d" % (k % 2))
             for mb in blocks:
                 for i in range(n0 // P, (n0 + count) // P):
                     at = place(mb, i)[1]
                     nc.tensor.transpose(ps[:, at : at + P], res[i][:, P * mb : P * (mb + 1)], ident32[:])
             nc.scalar.copy(res_t[:, k, :], ps[:])
 
-        def recall_half(s, picked, hf, tag):
+        make_damping(0)
+        for s in range(HEAD):
+            round_wa(s)
+            quantise_wa(s)
+        make_weight(0)
+        make_damping(1)
+        make_response(0)
+        base_cols = onto_partitions(base_rows, "base_cols", "B0")
+        make_response(1)
+        round_wa(HEAD)
+        for s in range(SLICES - 1):
+            put_states(s)
+            if s + 2 < SLICES:
+                quantise_wa(s + 2)
+            width = M if s < PASS_SLICES else HALF
+            picked = ring2.tile([P, M], F32, name="picked")
+            recall(s, picked[:, 0:width], 0, width)
+            make_weight(s + 1)
+            x = stage[s + 2][:, 2 * S : 3 * S]
+            bound(s, x[:, 0:width], picked[:, 0:width])
+            if s + 2 < SLICES:
+                make_damping(s + 2)
+                make_response(s + 2)
+                if s + 3 < SLICES:
+                    round_wa(s + 3)
+                else:
+                    open_stage(s + 3)
+            turn(s, x, x_t0 if s < PASS_SLICES else x_t1[0], width // P, "Y%d" % (s % 2))
+            if s == PASS_SLICES - 1:
+                for hf in range(2):
+                    turn_back(x_t0, 2 * hf, grouped0[:, PACK * HALF * hf : PACK * HALF * (hf + 1)], "U%d" % hf)
+                nc.vector.quantize_mx(out=x0_w[:].bitcast(FP8X4), scales=x0_s[:], in_=grouped0[:])
+        put_states(SLICES - 1)
+        for k in range(len(PIECES)):
+            turn_residual(k)
+
+        def recall_half(s, picked, hf, bank):
             recall(s, picked, HALF * hf, HALF * (hf + 1))
             x = ring3.tile([P, HALF], BF16, name="x_half")
             bound(s, x[:], picked)
-            turn(s, x, x_t1[hf], 2, tag)
+            turn(s, x, x_t1[hf], HALF // P, bank)
 
-        def quantise_half(i, tag):
-            grouped = keep.tile([P, 4 * HALF], BF16, name="grouped1", tag=tag, align_bytes=64)
-            turn_back(x_t1[i], 0, grouped[:], "U%d" % i)
-            nc.vector.quantize_mx(out=x1_w[i][:].bitcast(FP8X4), scales=x1_s[i][:], in_=grouped[:])
+        def quantise_half(hf):
+            grouped = keep.tile([P, PACK * HALF], BF16, name="grouped1%d" % hf, align_bytes=64)
+            turn_back(x_t1[hf], 0, grouped[:], "U%d" % hf)
+            nc.vector.quantize_mx(out=x1_w[hf][:].bitcast(FP8X4), scales=x1_s[hf][:], in_=grouped[:])
 
-        late = held("late", 0, [P, 4, HALF], F32)
-        recall_half(7, late[:, 0, :], 0, "B0")
-        quantise_half(0, "hold2")
-        for s in range(4, 7):
-            recall_half(s, late[:, s - 3, :], 1, "U0")
-        last = keep.tile([P, HALF], F32, name="last")
-        recall_half(7, last[:], 1, "B0")
+        late = keep.tile([P, PASS_SLICES + 1, HALF], F32, name="late", tag="behind_last_scatter")
+        recall_half(SLICES - 1, late[:, 0, :], 0, "B0")
+        quantise_half(0)
+        for s in range(PASS_SLICES, SLICES):
+            recall_half(s, late[:, s - PASS_SLICES + 1, :], 1, "U0" if s + 1 < SLICES else "B0")
 
-        y_t = keep.tile([P, len(pieces), 4 * P], F32, name="y_t", tag="wa_raw4")
+        y_t = keep.tile([P, len(PIECES), PASS], F32, name="y_t", tag="wa_raw%d" % (HEAD + 2))
 
-        def x_operand(a, mb):
+        def x_operand(a, m0, count):
             if a == 0:
-                return x0_w[:, P * mb : P * (mb + 1)], x0_s[:, P * mb : P * (mb + 1)]
-            cols_m = slice(P * (mb % 2), P * (mb % 2 + 1))
-            return x1_w[mb // 2][:, cols_m], x1_s[mb // 2][:, cols_m]
+                return x0_w[:, m0 : m0 + count], x0_s[:, m0 : m0 + count]
+            hf, lo = divmod(m0, HALF)
+            return x1_w[hf][:, lo : lo + count], x1_s[hf][:, lo : lo + count]
 
-        def product_turned(k, tag):
-            blocks, n0, count = pieces[k]
-            ps = psum.tile([P, 4 * P], F32, name="yt_ps", tag=tag)
+        def product_turned(k, bank):
+            blocks, n0, count = PIECES[k]
+            ps = psum.tile([P, PASS], F32, name="yt_ps", tag=bank)
             for j, mb in enumerate(blocks):
-                for a in PASS_ORDER:
-                    words, scales = x_operand(a, mb)
+                for a in range(R_PASSES):
+                    words, scales = x_operand(a, P * mb, P)
                     nc.tensor.matmul_mx(
                         out=ps[:, count * j : count * (j + 1)],
                         lhsT=words.bitcast(FP8X4),
                         lhsT_scale=scales,
                         rhs=wy_w[:, a, n0 : n0 + count].bitcast(FP8X4),
                         rhs_scale=wy_s[:, N * a + n0 : N * a + n0 + count],
-                        start=(a == PASS_ORDER[0]),
-                        stop=(a == PASS_ORDER[1]),
+                        start=(a == 0),
+                        stop=(a == R_PASSES - 1),
                     )
             nc.scalar.copy(y_t[:, k, :], ps[:])
 
@@ -413,10 +372,10 @@ def tile_list_trap_spray_scores_kernel(
             if hf == 1:
                 nc.sync.dma_start(out[P * i : P * (i + 1), :], outs[i][:])
 
-        def score_direct(i, tag):
-            ps = psum.tile([P, HALF], F32, name="y_ps", tag=tag)
-            for a in range(RP):
-                words, scales = (x0_w[:, 0:HALF], x0_s[:, 0:HALF]) if a == 0 else (x1_w[0][:], x1_s[0][:])
+        def score_direct(i):
+            ps = psum.tile([P, HALF], F32, name="y_ps", tag="Y%d" % i)
+            for a in range(R_PASSES):
+                words, scales = x_operand(a, 0, HALF)
                 nc.tensor.matmul_mx(
                     out=ps[:],
                     lhsT=wy_w[:, a, P * i : P * (i + 1)].bitcast(FP8X4),
@@ -424,31 +383,32 @@ def tile_list_trap_spray_scores_kernel(
                     rhs=words.bitcast(FP8X4),
                     rhs_scale=scales,
                     start=(a == 0),
-                    stop=(a == RP - 1),
+                    stop=(a == R_PASSES - 1),
                 )
             y = ring3.tile([P, HALF], F32, name="y")
             nc.vector.tensor_tensor(y[:], ps[:], res[i][:, 0:HALF], ALU.add)
             put_scores(i, 0, y)
 
-        def score_turned(i, hf, tag):
-            ps = psum.tile([P, 2, P], F32, name="sum_ps", tag=tag)
-            for j in range(2):
+        def score_turned(i, hf, bank):
+            ps = psum.tile([P, HALF // P, P], F32, name="sum_ps", tag=bank)
+            for j in range(HALF // P):
                 k, at = place(2 * hf + j, i)
-                nc.tensor.matmul(ps[:, j, :], res_t[:, k, at : at + P], ident32[:], start=True, stop=False, is_transpose=True)
-                nc.tensor.matmul(ps[:, j, :], y_t[:, k, at : at + P], ident32[:], start=False, stop=True, is_transpose=True)
+                for first, src in ((True, res_t), (False, y_t)):
+                    nc.tensor.matmul(
+                        ps[:, j, :], src[:, k, at : at + P], ident32[:], start=first, stop=not first, is_transpose=True
+                    )
             y = ring3.tile([P, HALF], F32, name="y")
             nc.scalar.copy(y[:], ps[:].rearrange("p j m -> p (j m)"))
             put_scores(i, hf, y)
 
-        score_direct(0, "Y0")
-        score_direct(1, "Y1")
+        for i in range(DIRECT):
+            score_direct(i)
         product_turned(0, "A0")
         product_turned(1, "A1")
-        quantise_half(1, "hold3")
-        for i in range(2, NT):
+        quantise_half(1)
+        for i in range(DIRECT, N_TILES):
             score_turned(i, 0, "Y%d" % (i % 2))
-        product_turned(2, "B1")
-        product_turned(3, "A0")
-        product_turned(4, "A1")
-        for i in range(NT):
-            score_turned(i, 1, ["B0", "U0"][i % 2])
+        for k, bank in ((2, "B1"), (3, "A0"), (4, "A1")):
+            product_turned(k, bank)
+        for i in range(N_TILES):
+            score_turned(i, 1, ("B0", "U0")[i % 2])

from contextlib import ExitStack

import concourse.mybir as mybir
from concourse.masks import make_identity

F32 = mybir.dt.float32
BF16 = mybir.dt.bfloat16
I32 = mybir.dt.int32
U32 = mybir.dt.uint32
U16 = mybir.dt.uint16
U8 = mybir.dt.uint8
FP8X4 = mybir.dt.float8_e4m3fn_x4
FP4X4 = mybir.dt.float4_e2m1fn_x4
ACT = mybir.ActivationFunctionType
ALU = mybir.AluOpType

K, T, S, H, N, M = 1536, 2048, 512, 1024, 768, 512
P = 128
PACK = 4
PASS = P * PACK
K_PASSES = K // PASS
R_PASSES = H // PASS
SLICES = H // P
PASS_SLICES = PASS // P
N_TILES = N // P
HALF = M // 2
HEAD = 2
DIRECT = 2
FLOPS = 2 * K * H * S * 2 + 2 * H * N * M

UPPER = (DIRECT * P, N - DIRECT * P)
PIECES = [([0],) + UPPER, ([1],) + UPPER, ([2, 3], 0, DIRECT * P), ([2],) + UPPER, ([3],) + UPPER]


def place(mb, i):
    for k, (blocks, n0, count) in enumerate(PIECES):
        if mb in blocks and n0 <= P * i < n0 + count:
            return k, count * blocks.index(mb) + P * i - n0


def tile_list_trap_spray_scores_kernel(
    tc, tab_words, tab_scales, wa, wd_words, wd_scales, gain, page0, wgs, base,
    wy_words, wy_scales, resid, page1, wgo, offs, offs2, offs3, offs4, out,
):
    nc = tc.nc
    with ExitStack() as ctx:
        keep = ctx.enter_context(tc.tile_pool(name="keep", bufs=1))
        ring2 = ctx.enter_context(tc.tile_pool(name="ring2", bufs=2))
        ring3 = ctx.enter_context(tc.tile_pool(name="ring3", bufs=3))
        psum = ctx.enter_context(tc.psum_pool(name="psum", bufs=1))

        def load_list(src, name):
            t = keep.tile([P, S // 16], U16, name=name)
            nc.sync.dma_start(t[:], src)
            return t

        def load_scales(scales, src):
            passes = src.shape[0]
            for q in range(4):
                nc.sync.dma_start(
                    scales[32 * q : 32 * q + 4, :].bitcast(I32).rearrange("r (a c) -> r a c", a=passes),
                    src[:, 4 * q : 4 * q + 4, :].bitcast(I32).rearrange("a r c -> r a c"),
                )

        def load_table(a, parts):
            t = keep.tile([P, T], U32, name="tab_w%d" % a)
            src = tab_words[a].rearrange("p t i -> p (t i)").bitcast(I32)
            step = T // parts
            for c in range(0, T, step):
                nc.sync.dma_start(t[:, c : c + step].bitcast(I32), src[:, c : c + step])
            return t

        def load_wa_pass(dst, a, s0):
            rows = wa[PASS * a : PASS * (a + 1), P * s0 : P * (s0 + 2)]
            nc.sync.dma_start(dst, rows.rearrange("(p j) c -> p j c", j=PACK))

        def load_wa_pair(s0):
            t = keep.tile([P, K_PASSES, PACK, 2 * P], F32, name="wa_raw%d" % s0)
            for a in range(K_PASSES):
                load_wa_pass(t[:, a], a, s0)
            return t

        def load_wd_words(s0, count):
            t = keep.tile([P, K_PASSES, 2 * P * count], U8, name="wd_w%d" % s0, align_bytes=64)
            src = wd_words[:, :, 2 * P * s0 : 2 * P * (s0 + count)].bitcast(I32)
            nc.sync.dma_start(t[:].bitcast(I32), src.rearrange("a p c -> p a c"))
            return t

        def load_wd_scales(s0, count):
            t = keep.tile([P, K_PASSES * P * count], U8, name="wd_s%d" % s0, align_bytes=64)
            nc.vector.memset(t[:].bitcast(I32), 0)
            load_scales(t, wd_scales[:, :, P * s0 : P * (s0 + count)])
            return t[:].rearrange("p (a c) -> p a c", a=K_PASSES)

        def load_vector(src, name):
            t = keep.tile([P, P], F32, name=name)
            nc.vector.memset(t[:], 0.0)
            nc.sync.dma_start(t[0:SLICES, :], src.rearrange("(s q) -> s q", q=P))
            return t

        def load_rows(src, i, name):
            t = keep.tile([P, src.shape[1]], F32, name=name)
            nc.sync.dma_start(t[:], src[P * i : P * (i + 1), :])
            return t

        tab_s = keep.tile([P, K_PASSES * T], U8, name="tab_s", align_bytes=64)
        wy_s = keep.tile([P, R_PASSES * N], U8, name="wy_s", align_bytes=64)
        nc.gpsimd.memset(tab_s[:, 0 : K_PASSES * T // 2].bitcast(I32), 0)
        nc.vector.memset(tab_s[:, K_PASSES * T // 2 : K_PASSES * T].bitcast(I32), 0)
        nc.vector.memset(wy_s[:].bitcast(I32), 0)

        ident32 = keep.tile([P, P], F32, name="ident32")
        make_identity(nc, ident32[:])
        ident16 = keep.tile([P, P], BF16, name="ident16")
        nc.scalar.copy(ident16[:], ident32[:])

        tab_w = [load_table(0, 4)]
        list1 = load_list(offs, "list1")
        list2 = load_list(offs2, "list2")
        list3 = load_list(offs3, "list3")
        tab_w.append(load_table(1, 1))
        load_scales(tab_s, tab_scales)
        tab_w.append(load_table(2, 1))
        wd_head_w = load_wd_words(0, HEAD)
        gain_rows = load_vector(gain, "gain_rows")
        wa_head = [keep.tile([P, PACK, HEAD * P], F32, name="wa_head%d" % a) for a in range(K_PASSES)]
        load_wa_pass(wa_head[0][:], 0, 0)
        wd_head_s = load_wd_scales(0, HEAD)
        for a in range(1, K_PASSES):
            load_wa_pass(wa_head[a][:], a, 0)
        base_rows = load_vector(base, "base_rows")
        wgs_t = load_rows(wgs, 0, "wgs_t")
        pages = [load_rows(page0, 0, "page0_0")]
        wa_raw = {}
        for s0 in range(HEAD, SLICES, 2):
            wa_raw[s0] = load_wa_pair(s0)
            if s0 == HEAD:
                wd_rest_w = load_wd_words(HEAD, SLICES - HEAD)
                wd_rest_s = load_wd_scales(HEAD, SLICES - HEAD)
            for s in (s0 - 1, s0):
                pages.append(load_rows(page0, s, "page0_%d" % s))
        pages.append(load_rows(page0, SLICES - 1, "page0_last"))
        wy_w = keep.tile([P, R_PASSES, N], U32, name="wy_w", align_bytes=64)
        nc.sync.dma_start(wy_w[:].bitcast(I32), wy_words.rearrange("a p c i -> p a (c i)").bitcast(I32))
        load_scales(wy_s, wy_scales)
        list4 = load_list(offs4, "list4")
        wgo_t = load_rows(wgo, 0, "wgo_t")
        res = [load_rows(resid, i, "res%d" % i) for i in range(N_TILES)]
        outs = [load_rows(page1, i, "page1_%d" % i) for i in range(N_TILES)]

        def onto_partitions(rows, name, bank):
            ps = psum.tile([P, P], F32, name="cols_ps", tag=bank)
            nc.tensor.transpose(ps[:], rows[:], ident32[:])
            cols = keep.tile([P, SLICES], F32, name=name)
            nc.scalar.copy(cols[:], ps[:, 0:SLICES])
            return cols

        gain_cols = onto_partitions(gain_rows, "gain_cols", "U0")

        v_s = [keep.tile([P, S], U8, name="v_s%d" % a, align_bytes=64) for a in range(K_PASSES)]
        v_w = [keep.tile([P, S], U32, name="v_w%d" % a, align_bytes=64) for a in range(K_PASSES)]
        for a in range(K_PASSES):
            nc.vector.tensor_copy(v_s[a][:], tab_s[:, a * T : (a + 1) * T].indirect(list1[:]))
        for a in range(K_PASSES):
            nc.vector.tensor_copy(v_w[a][:], tab_w[a][:].indirect(list1[:]))

        stage, wa_q, damps, resps, weights = {}, {}, {}, {}, {}

        def open_stage(s):
            stage[s] = ring2.tile([P, K_PASSES * PASS], BF16, name="stage", align_bytes=64)

        def front_of_stage(s):
            return stage[s][:, 0 : 2 * S].bitcast(F32)

        def round_wa(s):
            open_stage(s)
            if s < HEAD:
                for a in range(K_PASSES):
                    nc.vector.tensor_copy(
                        stage[s][:, PASS * a : PASS * (a + 1)].rearrange("p (c i j) -> p c j i", i=4, j=PACK),
                        wa_head[a][:, :, P * s : P * (s + 1)].rearrange("p j (c i) -> p c j i", i=4),
                    )
            else:
                c0 = P * (s % 2)
                nc.scalar.copy(
                    stage[s][:].rearrange("p (a c i j) -> p a c j i", a=K_PASSES, i=4, j=PACK),
                    wa_raw[s - s % 2][:, :, :, c0 : c0 + P].rearrange("p a j (c i) -> p a c j i", i=4),
                )

        def quantise_wa(s):
            codes = ring2.tile([P, K_PASSES * P], U32, name="wa_codes", align_bytes=64)
            scales = ring2.tile([P, K_PASSES * P], U8, name="wa_scales", align_bytes=64)
            cuts = [0, P, 2 * P, 3 * P] if s == 0 else [0, 2 * P, 3 * P]
            for lo, hi in zip(cuts, cuts[1:]):
                nc.vector.quantize_mx(
                    out=codes[:, lo:hi].bitcast(FP8X4), scales=scales[:, lo:hi], in_=stage[s][:, PACK * lo : PACK * hi]
                )
            wa_q[s] = (codes, scales)

        def make_damping(s):
            words, scales, c0 = (wd_head_w, wd_head_s, P * s) if s < HEAD else (wd_rest_w, wd_rest_s, P * (s - HEAD))
            ps = psum.tile([P, S], F32, name="b_ps", tag="A1" if s == HEAD + 1 else "B%d" % (s % 2))
            for a in range(K_PASSES):
                nc.tensor.matmul_mx(
                    out=ps[:],
                    lhsT=words[:, a, 2 * c0 : 2 * (c0 + P)].bitcast(FP4X4),
                    lhsT_scale=scales[:, a, c0 : c0 + P],
                    rhs=v_w[a][:].bitcast(FP8X4),
                    rhs_scale=v_s[a][:],
                    start=(a == 0),
                    stop=(a == K_PASSES - 1),
                )
            damp = ring2.tile([P, S], F32, name="damp")
            nc.scalar.activation(damp[:], ps[:], ACT.Abs)
            nc.scalar.activation(damp[:], damp[:], ACT.Exp, scale=-1.0)
            damps[s] = damp

        def make_response(s):
            codes, scales = wa_q[s]
            ps = psum.tile([P, S], F32, name="a_ps", tag="B0" if s == 0 else "A%d" % (s % 2))
            for a in range(K_PASSES):
                nc.tensor.matmul_mx(
                    out=ps[:],
                    lhsT=codes[:, P * a : P * (a + 1)].bitcast(FP8X4),
                    lhsT_scale=scales[:, P * a : P * (a + 1)],
                    rhs=v_w[a][:].bitcast(FP8X4),
                    rhs_scale=v_s[a][:],
                    start=(a == 0),
                    stop=(a == K_PASSES - 1),
                )
            resp = front_of_stage(0) if s == 0 else ring2.tile([P, S], F32, name="resp")
            nc.scalar.activation(resp[:], ps[:], ACT.Tanh)
            resps[s] = resp

        def make_weight(s):
            if s + 1 < SLICES:
                weight = front_of_stage(s + 1)
            else:
                weight = keep.tile([P, S], F32, name="weight_last", tag="behind_last_scatter")
            nc.vector.scalar_tensor_tensor(
                weight[:], damps[s][:], gain_cols[:, s : s + 1], wgs_t[:], ALU.mult, ALU.mult
            )
            weights[s] = weight

        def put_states(s):
            nc.vector.tensor_tensor(pages[s][:].indirect(list2[:]), resps[s][:], weights[s][:], ALU.mult)

        def recall(s, picked, lo, hi):
            nc.vector.tensor_copy(picked, pages[s][:].indirect(list3[:, lo // 16 : hi // 16]))

        def bound(s, x, picked):
            nc.vector.tensor_scalar(x, picked, base_cols[:, s : s + 1], None, ALU.max)

        def turn(s, x, x_t, blocks, bank):
            ps = psum.tile([P, blocks, P], BF16, name="turn_ps", tag=bank)
            for mb in range(blocks):
                nc.tensor.transpose(ps[:, mb, :], x[:, P * mb : P * (mb + 1)], ident16[:])
            c0 = P * (s % PASS_SLICES)
            nc.scalar.copy(x_t[:, :, c0 : c0 + P], ps[:])

        def turn_back(x_t, mb0, grouped, bank):
            words = x_t[:].bitcast(F32)
            ps = psum.tile([P, 2, 2, P], F32, name="back_ps", tag=bank)
            for mb in range(2):
                for u in range(2):
                    nc.tensor.transpose(ps[:, mb, u, :], words[:, mb0 + mb, u : 2 * P : 2], ident32[:])
            nc.scalar.copy(
                grouped.bitcast(F32).rearrange("p (b m u) -> p b m u", b=2, u=2),
                ps[:].rearrange("p b u m -> p b m u"),
            )

        grouped0 = keep.tile([P, PACK * M], BF16, name="grouped0", align_bytes=64)
        x_t0 = keep.tile([P, M // P, PASS], BF16, name="x_t0")
        x_t1 = [keep.tile([P, HALF // P, PASS], BF16, name="x_t1%d" % hf) for hf in range(2)]
        x0_w = keep.tile([P, M], U32, name="x0_w", align_bytes=64)
        x0_s = keep.tile([P, M], U8, name="x0_s", align_bytes=64)
        x1_w = [keep.tile([P, HALF], U32, name="x1_w%d" % hf, align_bytes=64) for hf in range(2)]
        x1_s = [keep.tile([P, HALF], U8, name="x1_s%d" % hf, align_bytes=64) for hf in range(2)]

        res_t = keep.tile([P, len(PIECES), PASS], F32, name="res_t", tag="wa_raw%d" % HEAD)

        def turn_residual(k):
            blocks, n0, count = PIECES[k]
            ps = psum.tile([P, PASS], F32, name="rt_ps", tag="B%d" % (k % 2))
            for mb in blocks:
                for i in range(n0 // P, (n0 + count) // P):
                    at = place(mb, i)[1]
                    nc.tensor.transpose(ps[:, at : at + P], res[i][:, P * mb : P * (mb + 1)], ident32[:])
            nc.scalar.copy(res_t[:, k, :], ps[:])

        make_damping(0)
        for s in range(HEAD):
            round_wa(s)
            quantise_wa(s)
        make_weight(0)
        make_damping(1)
        make_response(0)
        base_cols = onto_partitions(base_rows, "base_cols", "B0")
        make_response(1)
        round_wa(HEAD)
        for s in range(SLICES - 1):
            put_states(s)
            if s + 2 < SLICES:
                quantise_wa(s + 2)
            width = M if s < PASS_SLICES else HALF
            picked = ring2.tile([P, M], F32, name="picked")
            recall(s, picked[:, 0:width], 0, width)
            make_weight(s + 1)
            x = stage[s + 2][:, 2 * S : 3 * S]
            bound(s, x[:, 0:width], picked[:, 0:width])
            if s + 2 < SLICES:
                make_damping(s + 2)
                make_response(s + 2)
                if s + 3 < SLICES:
                    round_wa(s + 3)
                else:
                    open_stage(s + 3)
            turn(s, x, x_t0 if s < PASS_SLICES else x_t1[0], width // P, "Y%d" % (s % 2))
            if s == PASS_SLICES - 1:
                for hf in range(2):
                    turn_back(x_t0, 2 * hf, grouped0[:, PACK * HALF * hf : PACK * HALF * (hf + 1)], "U%d" % hf)
                nc.vector.quantize_mx(out=x0_w[:].bitcast(FP8X4), scales=x0_s[:], in_=grouped0[:])
        put_states(SLICES - 1)
        for k in range(len(PIECES)):
            turn_residual(k)

        def recall_half(s, picked, hf, bank):
            recall(s, picked, HALF * hf, HALF * (hf + 1))
            x = ring3.tile([P, HALF], BF16, name="x_half")
            bound(s, x[:], picked)
            turn(s, x, x_t1[hf], HALF // P, bank)

        def quantise_half(hf):
            grouped = keep.tile([P, PACK * HALF], BF16, name="grouped1%d" % hf, align_bytes=64)
            turn_back(x_t1[hf], 0, grouped[:], "U%d" % hf)
            nc.vector.quantize_mx(out=x1_w[hf][:].bitcast(FP8X4), scales=x1_s[hf][:], in_=grouped[:])

        late = keep.tile([P, PASS_SLICES + 1, HALF], F32, name="late", tag="behind_last_scatter")
        recall_half(SLICES - 1, late[:, 0, :], 0, "B0")
        quantise_half(0)
        for s in range(PASS_SLICES, SLICES):
            recall_half(s, late[:, s - PASS_SLICES + 1, :], 1, "U0" if s + 1 < SLICES else "B0")

        y_t = keep.tile([P, len(PIECES), PASS], F32, name="y_t", tag="wa_raw%d" % (HEAD + 2))

        def x_operand(a, m0, count):
            if a == 0:
                return x0_w[:, m0 : m0 + count], x0_s[:, m0 : m0 + count]
            hf, lo = divmod(m0, HALF)
            return x1_w[hf][:, lo : lo + count], x1_s[hf][:, lo : lo + count]

        def product_turned(k, bank):
            blocks, n0, count = PIECES[k]
            ps = psum.tile([P, PASS], F32, name="yt_ps", tag=bank)
            for j, mb in enumerate(blocks):
                for a in range(R_PASSES):
                    words, scales = x_operand(a, P * mb, P)
                    nc.tensor.matmul_mx(
                        out=ps[:, count * j : count * (j + 1)],
                        lhsT=words.bitcast(FP8X4),
                        lhsT_scale=scales,
                        rhs=wy_w[:, a, n0 : n0 + count].bitcast(FP8X4),
                        rhs_scale=wy_s[:, N * a + n0 : N * a + n0 + count],
                        start=(a == 0),
                        stop=(a == R_PASSES - 1),
                    )
            nc.scalar.copy(y_t[:, k, :], ps[:])

        def put_scores(i, hf, y):
            lo, hi = HALF * hf, HALF * (hf + 1)
            nc.vector.tensor_tensor(outs[i][:].indirect(list4[:, lo // 16 : hi // 16]), y[:], wgo_t[:, lo:hi], ALU.mult)
            if hf == 1:
                nc.sync.dma_start(out[P * i : P * (i + 1), :], outs[i][:])

        def score_direct(i):
            ps = psum.tile([P, HALF], F32, name="y_ps", tag="Y%d" % i)
            for a in range(R_PASSES):
                words, scales = x_operand(a, 0, HALF)
                nc.tensor.matmul_mx(
                    out=ps[:],
                    lhsT=wy_w[:, a, P * i : P * (i + 1)].bitcast(FP8X4),
                    lhsT_scale=wy_s[:, N * a + P * i : N * a + P * (i + 1)],
                    rhs=words.bitcast(FP8X4),
                    rhs_scale=scales,
                    start=(a == 0),
                    stop=(a == R_PASSES - 1),
                )
            y = ring3.tile([P, HALF], F32, name="y")
            nc.vector.tensor_tensor(y[:], ps[:], res[i][:, 0:HALF], ALU.add)
            put_scores(i, 0, y)

        def score_turned(i, hf, bank):
            ps = psum.tile([P, HALF // P, P], F32, name="sum_ps", tag=bank)
            for j in range(HALF // P):
                k, at = place(2 * hf + j, i)
                for first, src in ((True, res_t), (False, y_t)):
                    nc.tensor.matmul(
                        ps[:, j, :], src[:, k, at : at + P], ident32[:], start=first, stop=not first, is_transpose=True
                    )
            y = ring3.tile([P, HALF], F32, name="y")
            nc.scalar.copy(y[:], ps[:].rearrange("p j m -> p (j m)"))
            put_scores(i, hf, y)

        for i in range(DIRECT):
            score_direct(i)
        product_turned(0, "A0")
        product_turned(1, "A1")
        quantise_half(1)
        for i in range(DIRECT, N_TILES):
            score_turned(i, 0, "Y%d" % (i % 2))
        for k, bank in ((2, "B1"), (3, "A0"), (4, "A1")):
            product_turned(k, bank)
        for i in range(N_TILES):
            score_turned(i, 1, ("B0", "U0")[i % 2])
